import numpy as np, ml_dtypes
CORES = [6,15,38,47]
N = 4
import mx_ref
BF = ml_dtypes.bfloat16
def gentries(a):
    return np.ascontiguousarray(a.reshape(8, 16, -1).transpose(0, 2, 1)).reshape(8, -1)
def gtable(e):
    e = np.asarray(e); return np.ascontiguousarray(e.reshape(8, -1, 16).transpose(0, 2, 1)).reshape(128, -1).astype(np.int32)
def gcols(t, e):
    v = np.concatenate([t.reshape(8, 16, -1, 4), np.zeros((8, 16, 1, 4), BF)], axis=2)
    return np.ascontiguousarray(np.stack([v[g][:, e[g]] for g in range(8)])).reshape(128, -1)
def gpick(z, e):
    return np.concatenate([z[16 * g:16 * g + 16][:, e[g]] for g in range(8)])
def tile(rs):
    return np.stack(rs, axis=2).reshape(128, -1).astype(BF)
def pick(q, e):
    c = np.concatenate([q[0].reshape(128, -1, 4), np.zeros((128, 1, 4), np.uint8)], axis=1); s = np.concatenate([q[1], np.ones((16, 1), np.uint8)], axis=1)
    return (np.ascontiguousarray(c[:, e].reshape(128, -1)), np.ascontiguousarray(s[:, e]))
def join(*qs):
    return (np.concatenate([q[0] for q in qs], axis=1), np.concatenate([q[1] for q in qs], axis=1))
def put(q, e, v):
    c, s = q[0].reshape(128, -1, 4).copy(), q[1].copy(); c[:, e] = v[0].reshape(128, -1, 4); s[:, e] = v[1]
    return (c.reshape(128, -1), s)
def pk(c, s):
    return (np.ascontiguousarray(c), mx_ref.live(s))
def emit(q):
    return q[0], q[1]
def packed(v, rng):
    q = [mx_ref.quantize(np.ascontiguousarray(v[r])) for r in range(N)]
    return np.stack([a for a, b in q]), np.stack([mx_ref.plane(b, rng) for a, b in q])
def values_of_codes():
    e, c = np.zeros((128, 128, 4), np.float32), np.zeros((128, 2, 4), np.uint8)
    e[np.arange(128), np.arange(128), 0] = 1
    c[:127, :, 0] = np.arange(256).reshape(2, 128).T[:127]
    return mx_ref.matmul(mx_ref.quantize(e.reshape(128, 512).astype(BF)), (c.reshape(128, 8), np.full((16, 2), 127, np.uint8))).T.reshape(-1).astype(np.float64)
CODE_VALUE, SCALE_VALUE = values_of_codes(), 2.0 ** (np.arange(256) - 127.0)
def decode(q):
    return (CODE_VALUE[q[0]].reshape(16, 8, -1, 4) * SCALE_VALUE[q[1]][:, None, :, None] + 0.0).reshape(128, -1).astype(np.float32)
def f(rng, *shape):
    return mx_ref.flush((rng.standard_normal(shape, dtype=np.float32) * np.exp2(rng.integers(-2, 3, shape[:-1] + (1,)))).astype(BF))
def wide(rng, *shape, cols=0):
    v = rng.standard_normal(shape, dtype=np.float32) * np.exp2(rng.integers(-12, 13, shape)).astype(np.float32)
    if cols: v *= np.repeat(np.exp2(rng.integers(-cols, cols + 1, shape[:-2] + (1, shape[-1] // 4))) * (rng.random(shape[:-2] + (1, shape[-1] // 4)) > 0.0625), 4, axis=-1).astype(np.float32)
    return mx_ref.flush(v.astype(BF))
C, E, B, K, R = 400, 20, 4, 80, 3
STEP = [1, 2, 1]
LO, HI = 3, 5
def gaps(p):
    return np.argmin(p[::16].reshape(8, E, E) + np.float32(0.0), axis=2)
def starts(a, c):
    s, free = np.full(a.shape, -1), np.zeros(c.shape, int)
    for k in range(B):
        n = a[:, :, k]
        i = np.where((c >= free) & (c < free + n), c + 1, free)
        fits = i + n <= E
        s[:, :, k] = np.where(fits, i, -1)
        free = np.where(fits, i + n + 1, free)
    return s
def solve(a, c):
    left = starts(a, c)
    m = starts(a[:, :, ::-1], E - 1 - c)[:, :, ::-1]
    end = E - 1 - m
    first, last = np.maximum(left, end - a + 1), np.minimum(left + a - 1, end)
    sure = (left >= 0) & (m >= 0) & (first <= last)
    line = E * np.arange(E)[None, :, None]
    return np.where(sure, line + left, -1).reshape(8, K), np.where(sure, line + end, -1).reshape(8, K), np.where(sure, first, -1), np.where(sure, last, -1)
def fallen(first, last):
    cell = np.arange(E)
    inside = (cell >= first[:, :, :, None]) & (cell <= last[:, :, :, None])
    e = np.where(inside.any(axis=2), B * cell[None, :, None] + np.argmax(inside, axis=2), -1)
    return np.ascontiguousarray(e.transpose(0, 2, 1)).reshape(8, C)
def numbers_of(rng):
    return {"x": np.array(f(rng, N, 128, 4 * C)), "u": np.array(f(rng, N, 128, 512)), "v": np.array(f(rng, N, 128, 512))}
def weights(rng, still=[]):
    w = np.array(f(rng, N, 128, 2048)).reshape(N, 8, 16, 4, 8, 16, 4)
    for i in still:
        w[:, :, i] = 0
        w[:, :, :, :, :, i] = 0
    c, p = packed(w.reshape(N, 128, 2048), rng)
    return {"wc": c, "ws": p}
def lengths(rng):
    return rng.integers(LO, HI + 1, (N, 8, E, B))
def blocks(a):
    return {"bl": np.stack([gtable(a[r].reshape(8, K)) for r in range(N)])}
def signs(rng):
    return np.stack([rng.permutation(8) % 2 * 2.0 - 1.0 for r in range(N)])
def setup_inputs(rng):
    return {**numbers_of(rng), **weights(rng), **blocks(lengths(rng))}
def setup_inputs_ties(rng):
    d = numbers_of(rng)
    e = rng.permutation(N)
    x = d["x"].reshape(N, 8, 16, C, 4)
    for r in range(N):
        for g in range(8):
            k = np.zeros(C, int) if r == e[0] else rng.permutation(C) % 3
            a = x[r, g, :8, :3].copy()
            a[:, 2] = 0
            x[r, g, :8] = a[:, k]
    x[e[1]] = 0
    u = d["u"].reshape(N, 8, 16, 8, 16, 4)
    k = u.copy()
    u[:, :, :, :, 0] = 0
    for g in range(8): u[:, g, :8, g, 0] = k[:, g, :8, g, 0]
    return {"x": x.reshape(N, 128, 4 * C), "u": u.reshape(N, 128, 512), "v": d["v"], **weights(rng, range(8)), **blocks(lengths(rng))}
def setup_inputs_near(rng):
    d = numbers_of(rng)
    x = d["x"].astype(np.float32).reshape(N, 8, 16, C, 4)
    u = d["u"].reshape(N, 128, 128, 4)
    u[:, :, ::16] = 0
    x[:, :, 0] = 0
    o, c, far = rng.permutation(N) % 4, signs(rng), signs(rng)
    j = np.arange(E)
    for r in range(N):
        i = (j + rng.integers(0, E, (8, E, 1))) % E
        twos = rng.integers(0, 2, (8, E, 1)) > 0
        if o[r] == 3:
            i = i % (E // 2) * 2 + j // (E // 2)
            twos = twos | True
        s = (np.where(twos, (E - 1 - i) // 2, E - 1 - i) + rng.integers(1, 200, (8, E, 1))).reshape(8, C)
        i = i.reshape(8, C)
        size = 1.0 if o[r] < 2 else 2.0 ** -4
        g = ((s[:, :, None] >> np.arange(8)) & 1) * np.exp2(np.arange(8) - 23.0) * size
        x[r, :, 8:] = rng.integers(4, 8, (8, 8, C, 4)) * 2.0 ** -20 * size
        x[r, :, 8] = g[:, :, :4]
        x[r, :, 9] = g[:, :, 4:]
        if o[r] < 2: x[r, :, 0, :, 0] = np.where((i == 0) & (far[r][:, None] > 0), 2.0 ** 30, c[r][:, None])
        if o[r] == 3:
            x[r, :, 10] = 0
            x[r, :, 10, :, 0] = (9 - i % 2) * 2.0 ** -30
        k = 1.0 if o[r] == 0 else 2.0 ** -30
        for h in range(0, 128, 16):
            u[r, h, h, 0] = k
            u[r, h + 8:h + 10, h] = k
            if o[r] == 3: u[r, h + 10, h, 0] = k
    return {"x": x.reshape(N, 128, 4 * C).astype(BF), "u": u.reshape(N, 128, 512), "v": d["v"], **weights(rng, [0, 8, 9, 10, 11, 12, 13, 14, 15]), **blocks(lengths(rng))}
def setup_inputs_huge(rng):
    d = numbers_of(rng)
    c = np.stack([rng.permutation(C) % 2 * 2.0 - 1.0 for r in range(N)])
    c[rng.permutation(N) < N // 2] = 1
    x = 2.0 ** 30 * (0.55 + 0.15 * rng.random((N, 128, C, 4))) * c[:, None, :, None]
    u = d["u"].reshape(N, 128, 128, 4)
    a = 2.0 ** 30 * (1 - 0.25 * rng.random((N, 128, 8, 4))) * signs(rng)[:, None, :, None]
    u[:, :, ::16] = a.astype(np.float32).astype(BF)
    w = np.zeros((N, 128, 4, 128, 4), np.float32)
    i = np.arange(128)
    for b in range(4): w[:, i, b, i, b] = -1
    wc, ws = packed(w.reshape(N, 128, 2048).astype(BF), rng)
    return {"x": x.astype(np.float32).reshape(N, 128, 4 * C).astype(BF), "u": u.reshape(N, 128, 512), "v": d["v"], "wc": wc, "ws": ws, **blocks(lengths(rng))}
def setup_inputs_packs(rng):
    d = numbers_of(rng)
    x = d["x"].reshape(N, 8, 16, C, 4)
    u = d["u"].reshape(N, 128, 128, 4)
    a = lengths(rng)
    gap = np.where(rng.random((N, 8, E)) < 0.25, rng.integers(0, 2, (N, 8, E)) * (E - 1), rng.integers(0, E, (N, 8, E)))
    ends = np.sort(np.argsort(rng.random((N, 8, E, E - B)), axis=3)[:, :, :, :B - 1], axis=3) + 1
    full = np.diff(ends, axis=3, prepend=0, append=E - B + 1)
    between = np.take_along_axis(ends + np.arange(B - 1), rng.integers(0, B - 1, (N, 8, E, 1)), axis=3)[:, :, :, 0]
    e = rng.permutation(N)
    long = np.arange(E)
    long = long[long % 4 < 2]
    for r in range(N):
        h = rng.permutation(8)
        a[r, h[0]] = 1
        a[r, h[1]] = E
        a[r, h[2]] = 1
        a[r, h[2], ::2, 0] = E - 1
        a[r, h[2], 1::2, B - 1] = E - 1
        a[r, h[2], long] = E
        a[r, h[2], long, long % 2 * (B - 1)] = E - 1
        gap[r, h[2], long] = (long // 4 + rng.integers(2)) % 2 * (E - 1)
        a[r, h[3]] = E // 2
        a[r, h[4]] = rng.integers(1, E + 1, (E, B))
        a[r, h[5]] = full[r, h[5]]
        gap[r, h[5], ::2] = between[r, h[5], ::2]
        a[r, h[6]] = E // B
    a[e[0]] = E
    a[e[1]] = full[e[1]]
    gap[e[1]] = between[e[1]]
    z = rng.integers(0, 2, (N, 8, E, E))
    np.put_along_axis(z, gap[:, :, :, None], -1, axis=3)
    x[:, :, 0, :, 0] = z.reshape(N, 8, C).astype(np.float32).astype(BF)
    u[:, :, ::16] = 0
    for h in range(0, 128, 16): u[:, h, h, 0] = 1
    return {"x": x.reshape(N, 128, 4 * C), "u": u.reshape(N, 128, 512), "v": d["v"], **weights(rng, [0]), **blocks(a)}
def setup_inputs_spread(rng):
    d = setup_inputs(rng)
    d["x"] = wide(rng, N, 128, 4 * C, cols=6)
    return d
def check_inputs(d):
    b = []
    for k in ("x", "u", "v"):
        a = np.abs(d[k].astype(np.float32))
        if not (np.isfinite(a).all() and ((a == 0) | (a >= 2.0 ** -30) & (a <= 2.0 ** 30)).all()): b.append("a value of " + k)
    if ((d["wc"] & 0x7F) == 0x7F).any(): b.append("a code of wc that is no number")
    none, least, most = [emit(mx_ref.quantize(np.full((128, 16), k, np.float32).astype(BF)))[1][0, 0] for k in (0.0, 2.0 ** -30, 2.0 ** 30)]
    for r in range(N):
        s = mx_ref.live(d["ws"][r])
        if ((s != none) & ((s < least) | (s > most))).any(): b.append("a scale of ws")
    if ((d["bl"] < 1) | (d["bl"] > E)).any(): b.append("a length in bl")
    return b
def reference(x, u, v, wc, ws, bl):
    qu = [mx_ref.quantize(u[r]) for r in range(N)]
    lay = [pk(wc[r], ws[r]) for r in range(N)]
    size = [gentries(bl[r]).reshape(8, E, B).astype(int) for r in range(N)]
    now = [x[r] for r in range(N)]
    for t in range(R):
        own, sent, bound = [], [], []
        for r in range(N):
            q = mx_ref.quantize(now[r])
            a = decode(q).astype(BF)
            e, h, first, last = solve(size[r], gaps(mx_ref.matmul(qu[r], q)))
            z = ((gcols(a, e).astype(np.float32) + gcols(a, h).astype(np.float32)) * np.float32(0.5)).astype(BF)
            own.append(a)
            sent.append(mx_ref.quantize(z))
            bound.append((first, last))
        for r in range(N):
            p = r ^ STEP[t]
            e = fallen(bound[p][0], bound[p][1])
            made = []
            for b in range(4):
                h = mx_ref.matmul(pick(lay[r], np.arange(128 * b, 128 * b + 128)), sent[p]) * np.float32(0.03125)
                h = np.concatenate([h, np.zeros((128, 1), np.float32)], axis=1)
                made.append(own[r][:, b::4].astype(np.float32) + gpick(h, e))
            now[r] = tile(made)
    y, ob = np.zeros((N, 128, C), np.float32), np.zeros((N, 8, 2 * K), np.float32)
    oc, osc = np.zeros((N, 128, 4 * C), np.uint8), np.zeros((N, 16, C), np.uint8)
    for r in range(N):
        q = mx_ref.quantize(now[r])
        y[r] = mx_ref.matmul(mx_ref.quantize(v[r]), q)
        ob[r] = np.stack([bound[r][0], bound[r][1]], axis=3).reshape(8, 2 * K)
        oc[r], osc[r] = emit(q)
    return {"y": y, "ob": ob, "oc": oc, "osc": osc}

@@ -1,0 +1,444 @@
+from concourse.mybir import dt, AluOpType as A, ActivationFunctionType as F
+
+C, K, R = 400, 80, 3
+STEP = [1, 2, 1]
+BIG = 1e29
+Q4, U8, BF, F32, I32, U16 = "float8_e4m3fn_x4", "uint8", "bfloat16", "float32", "int32", "uint16"
+SCRATCH = {}
+for _d, _l in (
+    (BF, "xin 1600 xn 1600 uin 512 vin 512 ones 128 eb 516 zt 512 mz 320 th 1616 t01 800 reset 200 nn 400 key 400 vv 400 n1g 20 ng0 20 ng1 20 "
+         "snd0 88 snd1 88 snd2 88 lb0 80 lb1 80 lb2 80"),
+    (Q4, "qx 400 qu 128 qu2 128 qv 128 qw 512 qe 512 lq0 208 lq1 208 lq2 208"),
+    (U8, "sx 400 su 128 su2 128 sv 128 sw 512 se 512 ls0 208 ls1 208 ls2 208"),
+    (I32, "bli 8 pi 1 qi 3 upi 8"),
+    (U16, "upo 8 blo 8 lno 10 nlo 40 plo 4 glo 16 olo 10 el 26 zl 40 oo 40"),
+    (F32, "hh 800 g2 400 g3 400 yt 400 ex 400 qf 3 cola 8 colb 8 tab 32 t16 160 lift 256 il 10 xg 10 ln 10 a80 80 c640 640 hn 640 npk 40 "
+          "ns 80 n1 80 ta 80 d0a 240 c1 40 iz 20 iz2 40 flp 48 flg 256 flo 160 wsc 256 ii 500 ge 125 gt 125 jj 256 val 256 "
+          "nf 256 gs 256 cand 160 hs 160 aa 60 oa 61 bb 320 u0r 48 r1r 40 yy 80 x1 40 sm 60 fe 48 f1 60 w1 40 ww 40 o1 120 o2 40 orep 640 obt 160"),
+):
+    _w = _l.split()
+    for _i in range(0, len(_w), 2):
+        SCRATCH[_w[_i]] = ("sbuf", [128, int(_w[_i + 1])], _d)
+for _b in range(4):
+    SCRATCH["pd%d" % _b] = ("psum", [128, 512], F32)
+    SCRATCH["ph%d" % _b] = ("psum", [128, 512], F32)
+SEMAPHORES = ["cv", "ca", "cg", "sent", "rn0", "rn1"] + ["r%s%d" % (n, t) for n in "bcs" for t in range(R)] + ["s%d" % i for i in range(128)]
+
+
+def rank_program(g, core, T, topo):
+    rank = T.rank_of(core)
+    if rank is None:
+        return
+    V, S, P, Y = g.vector, g.scalar, g.tensor, g.sync
+    qs = {"v": V, "a": S, "p": P, "y": Y, "g": g}
+    total, seen, pend, nxt = {}, {}, {"v": [], "a": [], "g": []}, [0]
+
+    def tok():
+        nxt[0] += 1
+        return "s%d" % (nxt[0] - 1)
+
+    def op(q, ins, sem=None, n=1):
+        sem = sem or "c" + q
+        ins.then_inc(T.sem[sem], n)
+        total[sem] = total.get(sem, 0) + n
+        if q in pend and n == 1 and sem not in pend[q]:
+            pend[q].append(sem)
+        return sem
+
+    def wait(q, *sems):
+        for s in sems:
+            if seen.get((q, s), 0) < total[s]:
+                qs[q].wait_ge(T.sem[s], total[s])
+                seen[(q, s)] = total[s]
+
+    def bar(q):
+        wait(q, *pend[q])
+        pend[q][:] = []
+
+    def ms(ap, c, sem=None):
+        return op("v", V.memset(ap, c), sem)
+
+    def ts(out, a, s1, o1, s2=None, o2=None, sem=None):
+        return op("v", V.tensor_scalar(out, a, s1, None, o1) if o2 is None else V.tensor_scalar(out, a, s1, s2, o1, o2), sem)
+
+    def tt(out, a, b, o, sem=None):
+        return op("v", V.tensor_tensor(out, a, b, o), sem)
+
+    def cp(out, a, sem=None):
+        return op("v", V.tensor_copy(out, a), sem)
+
+    def scan(out, a, b, o0, o1, init=0.0, sem=None):
+        return op("v", V.tensor_tensor_scan(out, a, b, init, o0, o1), sem)
+
+    def quant(q, s, a, sem=None):
+        return op("v", V.quantize_mx(q, s, a), sem)
+
+    def act(out, a, scale=1.0, bias=0.0, func=F.Identity, sem=None):
+        return op("a", S.activation(out, a, func, bias=bias, scale=scale), sem)
+
+    def zero(out, n, sem):
+        return act(out, T.key[:, 0:n], 0.0, sem=sem)
+
+    def iota(out, pattern, base, sem, ch=0, whole=False):
+        if whole:
+            return op("g", g.iota(out, pattern, base, ch), sem)
+        return op("g", g.iota(out, pattern, base, ch, allow_small_or_imprecise_dtypes=True), sem)
+
+    def mm(out, lq, ls, rq, rs):
+        return op("p", P.matmul_mx(out, lq, ls, rq, rs, True, True), tok())
+
+    def dma(q, out, a, sem=None):
+        return op(q, qs[q].dma_start(out, a), sem or tok(), 16)
+
+    def send(out, a, sem, dst):
+        rid, pid, _ = topo.addr(dst)
+        g.remote_dma(out, a, T.sem[sem], T.sem.sent, pid, rid, topo.mask(core, dst))
+        total["sent"] = total.get("sent", 0) + len(topo.engines(core, dst))
+        total[sem] = len(topo.engines(dst, core))
+
+    def wrap(out, full, n, sem=None):
+        scan(T.wsc[:, 0:n], T.lift[:, 0:n], full, A.add, A.max)
+        bar("v")
+        return ts(out, T.wsc[:, 15:n:16], T.cola[:, 1:2], A.subtract, sem=sem)
+
+    db = dma("a", T.bli[:, 0:5], T.bl[:])
+    du = dma("a", T.uin[:], T.u[:])
+    dx = [dma("y", T.xin[:, 800 * h:800 * h + 800], T.x[:, 800 * h:800 * h + 800]) for h in range(2)]
+    dw = dma("y", T.qw[:].bitcast(dt.uint8), T.wc[:])
+    dma("y", T.sw[:], T.ws[:], dw)
+    dv = dma("y", T.vin[:], T.v[:])
+
+    k0, k1, k2, k3, k4, k5, k6, k7 = [tok() for _ in range(8)]
+    iota(T.pi[:], [[0, 1]], 0, k0, ch=1, whole=True)
+    iota(T.upi[:], [[16, 8]], 0, k0, whole=True)
+    iota(T.il[:, 0:5], [[4, 5]], 0, k0)
+    iota(T.il[:, 5:10], [[-4, 5]], 20, k0)
+    iota(T.tab[:], [[1, 32]], 0, k1)
+    iota(T.t16[:], [[0, 10], [1, 16]], 0, k2)
+    ko = ms(T.ones[:], 1.0, tok())
+    ms(T.eb[:], 0.0, ko)
+    ms(T.flp[:], 0.0, ko)
+    wait("g", ko)
+    op("g", g.affine_select(T.eb[:, 3:515:4], T.ones[:], [[1, 128]], A.is_equal, 0.0, 0, -1), k3)
+    iota(T.flp[:, 0:40], [[-20, 4], [2, 10]], 60, k5)
+    iota(T.key[:], [[0, 20], [-1, 20]], 32, k4)
+    iota(T.iz[:], [[0, 4], [80, 5]], -400, k7)
+
+    wait("v", k0)
+    ts(T.qi[:, 0:1], T.pi[:], 15, A.bitwise_and)
+    ts(T.qi[:, 1:2], T.pi[:], 2, A.logical_shift_right, 3, A.bitwise_and)
+    ts(T.qi[:, 2:3], T.pi[:], 3, A.bitwise_and)
+    kup = cp(T.upo[:], T.upi[:], tok())
+    bar("v")
+    kq = cp(T.qf[:], T.qi[:], tok())
+    ms(T.reset[:], 0.0)
+    bar("v")
+    qc, rc, bc = T.qf[:, 0:1], T.qf[:, 1:2], T.qf[:, 2:3]
+    ts(T.ln[:, 0:10:2], T.il[:, 0:5], rc, A.add)
+    ts(T.xg[:, 0:5], T.il[:, 5:10], qc, A.add)
+    ms(T.reset[:, 0:200:20], BIG)
+    wait("v", k2)
+    kt = ms(T.t16[:, 0:160:16], -1000.0, tok())
+    bar("v")
+    ts(T.xg[:, 5:10], T.xg[:, 0:5], 20.0, A.is_ge, -20.0, A.mult)
+    ms(T.ex[:, 0:400:200], BIG)
+    bar("v")
+    tt(T.ln[:, 1:10:2], T.xg[:, 0:5], T.xg[:, 5:10], A.add)
+    wait("v", db)
+    kb = cp(T.blo[:, 0:5], T.bli[:, 0:5], tok())
+    bar("v")
+    knl = tok()
+    for k in range(4):
+        ts(T.nlo[:, 10 * k:10 * k + 10], T.ln[:], 4.0, A.mult, float(3 - k), A.add, knl)
+    ts(T.lno[:], T.ln[:], 20.0, A.mult, 19.0, A.add)
+    wait("v", k3)
+    ke = tok()
+    for b in range(4):
+        quant(T.qe[:, 128 * b:128 * b + 128], T.se[:, 128 * b:128 * b + 128], T.eb[:, 3 - b:515 - b], ke)
+    wait("v", du)
+    kqu = quant(T.qu[:], T.su[:], T.uin[:], tok())
+    bar("v")
+    kpu = cp(T.qu2[:].bitcast(dt.uint32), T.qu[:].bitcast(dt.uint32).indirect(T.upo[:]), tok())
+
+    wait("a", kq)
+    kc = tok()
+    act(T.cola[:, 0:1], qc, -2048.0, -1024.0, sem=kc)
+    act(T.cola[:, 1:2], qc, -32.0, 480.0, F.Square, kc)
+    act(T.cola[:, 2:3], rc, 20.0, -1.0, sem=kc)
+    act(T.cola[:, 3:4], bc, 1.0, 1600.0, sem=kc)
+    act(T.cola[:, 4:5], qc, 2.0, 0.0, sem=kc)
+    bar("a")
+    act(T.colb[:, 0:1], T.cola[:, 1:2], -1.0, 0.0, sem=kc)
+    act(T.colb[:, 1:2], T.cola[:, 1:2], 1.0, 45.0, sem=kc)
+    act(T.colb[:, 2:3], T.cola[:, 1:2], 1.0, 67.0, sem=kc)
+    act(T.colb[:, 3:4], T.cola[:, 2:3], 1.0, -1.0, sem=kc)
+    wait("a", kt)
+    act(T.lift[:, 0:160], T.t16[:], 2048.0, T.cola[:, 0:1], sem=kc)
+    wait("a", k1, kb)
+    act(T.a80[:], T.tab[:].indirect(T.blo[:, 0:5]))
+    bar("a")
+    wait("a", knl)
+    kc6 = act(T.c640[:], T.a80[:].indirect(T.nlo[:]), sem=tok())
+    wait("a", kup, kqu)
+    ksu = op("a", S.activation(T.su2[:], T.su[:].indirect(T.upo[:]), F.Copy), tok())
+    wait("a", k4)
+    kn = tok()
+    for ap, n in ((T.d0a[:, 0:240:3], 80), (T.d0a[:, 2:240:3], 80), (T.aa[:, 2:60:3], 20), (T.oa[:, 0:1], 1), (T.bb[:, 0:60:3], 20)):
+        zero(ap, n, kn)
+    wait("v", kc, k5)
+    wrap(T.plo[:, 0:3], T.flp[:], 48)
+
+    xs = T.xin
+    for t in range(R):
+        dst = T.cores[rank ^ STEP[t]]
+        lq, ls, lb, ab = [T["%s%d" % (n, t)] for n in ("lq", "ls", "lb", "snd")]
+
+        if t == 0:
+            wait("p", kpu, ksu)
+        else:
+            bar("v")
+        ks, sb = [], [T.ph3, T.ph2]
+        for h in range(2):
+            if t == 0:
+                wait("v", dx[h])
+            q, s_ = T.qx[:, 200 * h:200 * h + 200], T.sx[:, 200 * h:200 * h + 200]
+            wait("p", quant(q, s_, xs[:, 800 * h:800 * h + 800], tok()))
+            ks.append(mm(sb[h][:, 0:200], T.qu2[:], T.su2[:], q, s_))
+        if t == 0:
+            wait("p", ke)
+        kd = [mm(T["pd%d" % b][:, 0:C], T.qe[:, 128 * b:128 * b + 128], T.se[:, 128 * b:128 * b + 128], T.qx[:], T.sx[:]) for b in range(4)]
+
+        if t == 0:
+            wait("v", kc6)
+            khn = tok()
+            for k in range(4):
+                scan(T.hn[:, 160 * k:160 * k + 160], T.lift[:, 0:160], T.c640[:, 160 * k:160 * k + 160], A.add, A.max, sem=khn)
+            wait("a", khn, k7)
+            nfx = T.colb[:, 0:1]
+            act(T.npk[:], T.hn[:, 15:640:16], 1.0, nfx)
+            act(T.ns[:, 1:80:2], T.hn[:, 15:640:16], 1.0, nfx)
+            for s in range(4):
+                act(T.ns[:, 20 * s:20 * s + 20:2], T.hn[:, 160 * (3 - s) + 15:160 * (4 - s):16], 1.0, nfx)
+            kng = act(T.n1g[:], T.hn[:, 31:640:32], 1.0, nfx, sem=tok())
+            bar("a")
+            act(T.n1[:], T.ns[:], 1.0, 1.0, sem=kn)
+            act(T.ta[:], T.ns[:], -1.0, 32.0, sem=kn)
+            act(T.d0a[:, 1:240:3], T.ns[:], 1.0, 34.0, sem=kn)
+            kn2 = act(T.iz2[:, 0:20], T.iz[:], 1.0, T.cola[:, 2:3], sem=tok())
+            act(T.iz2[:, 20:40], T.iz[:], 1.0, T.colb[:, 3:4], sem=kn2)
+            iota(T.ii[:, 0:125], [[0, 5], [-4, 5], [0, 5]], 20, k6)
+            iota(T.ii[:, 125:250], [[4, 5], [1, 5], [0, 5]], 0, k6)
+            iota(T.ii[:, 250:375], [[0, 5], [-8, 5], [-40, 5]], 201, k6)
+            iota(T.ii[:, 375:500], [[0, 5], [1, 5], [-5, 5]], 20, k6)
+            wait("g", kng)
+            for j in range(2):
+                send(T["ng%d" % j][:], T.n1g[:], "rn%d" % j, T.cores[rank ^ STEP[j]])
+            kfo = iota(T.flo[:], [[4, 20], [-80, 4], [320, 2]], 240, tok())
+        bar("a")
+        kth = tok()
+        for b in range(2):
+            wait("a", kd[b])
+            act(T.th[:, b:1600:4], T["pd%d" % b][:, 0:C], 0.5, sem=kth)
+
+        for h in range(2):
+            wait("v", ks[h])
+            scan(T.ex[:, 200 * h + 1:200 * h + 200], sb[h][:, 0:199], T.reset[:, 1:200], A.min, A.add, BIG)
+        bar("v")
+        for h in range(2):
+            tt(T.nn[:, 200 * h:200 * h + 200], sb[h][:, 0:200], T.ex[:, 200 * h:200 * h + 200], A.is_ge)
+        if t == 0:
+            wait("v", k4)
+        bar("v")
+        scan(T.vv[:], T.nn[:], T.key[:], A.mult, A.max)
+        bar("v")
+        cp(T.cand[:], T.vv[:].indirect(T.lno[:]))
+        bar("v")
+        khs = scan(T.hs[:], T.lift[:, 0:160], T.cand[:], A.add, A.max, sem=tok())
+        bar("v")
+        hs = T.hs[:, 15:160:16]
+        ts(T.bb[:, 2:60:6], hs, T.cola[:, 1:2], A.subtract)
+        ts(T.bb[:, 5:60:6], hs, -1.0, A.mult, T.colb[:, 1:2], A.add)
+        wait("a", khs)
+        krp = tok()
+        for k in range(4):
+            act(T.u0r[:, 10 * k:10 * k + 10], hs, 1.0, T.colb[:, 0:1], sem=krp)
+            act(T.r1r[:, 10 * k:10 * k + 10], hs, -1.0, T.colb[:, 2:3], sem=krp)
+        if t == 0:
+            zero(T.u0r[:, 40:48], 8, krp)
+            zero(T.th[:, 1600:1616], 16, kth)
+            zero(T.zt[:, 320:512], 192, kth)
+            wait("v", kn)
+        for b in range(2, 4):
+            wait("a", kd[b])
+            act(T.th[:, b:1600:4], T["pd%d" % b][:, 0:C], 0.5, sem=kth)
+
+        for s in range(4):
+            bar("v")
+            u = T.bb[:, 60 * s + 2:60 * s + 60:3]
+            tt(T.aa[:, 1:60:3], u, T.n1[:, 20 * s:20 * s + 20], A.add)
+            tt(T.aa[:, 0:60:3], u, T.ta[:, 20 * s:20 * s + 20], A.is_gt)
+            if s == 0:
+                ts(T.bb[:, 300:320], u, 21.0, A.add)
+            bar("v")
+            scan(T.oa[:, 1:61], T.d0a[:, 60 * s:60 * s + 60], T.aa[:], A.mult, A.max)
+            bar("v")
+            tt(T.bb[:, 60 * s + 1:60 * s + 60:3], T.oa[:, 2:61:3], T.bb[:, 300:320], A.is_le)
+            bar("v")
+            scan(T.bb[:, 60 * s + 60:60 * s + 120], T.oa[:, 0:60], T.bb[:, 60 * s:60 * s + 60], A.mult, A.max)
+        bar("v")
+        tt(T.yy[:], T.bb[:, 62:300:3], T.bb[:, 1:240:3], A.mult)
+        nz = T.npk[:, 0:40:2]
+        if t == 0:
+            wait("v", kn2)
+            tt(T.c1[:, 0:20], T.iz2[:, 0:20], nz, A.subtract)
+            tt(T.c1[:, 20:40], T.iz2[:, 20:40], nz, A.add)
+        bar("v")
+        wait("v", krp)
+        ksn = tok()
+        tt(ab[:, 40:88], T.yy[:].indirect(T.plo[:, 0:3]), T.u0r[:], A.subtract, ksn)
+        tt(ab[:, 0:40], T.r1r[:], T.yy[:, 1:80:2], A.subtract, ksn)
+        wait("g", ksn)
+        send(lb[:], ab[:, 0:80], "rb%d" % t, dst)
+        bar("v")
+        az, sz_, ok1, ok2, ok = ab[:, 40:80:2], ab[:, 0:40:2], T.sm[:, 0:20], T.sm[:, 20:40], T.sm[:, 40:60]
+        tt(T.x1[:, 0:20], az, T.c1[:, 0:20], A.add)
+        tt(T.x1[:, 20:40], sz_, T.c1[:, 20:40], A.add)
+        tt(ok1, az, sz_, A.is_gt)
+        bar("v")
+        tt(ok2, T.x1[:, 0:20], T.x1[:, 20:40], A.is_le)
+        tt(T.w1[:, 0:20], T.x1[:, 0:20], ok1, A.mult)
+        tt(T.w1[:, 20:40], T.x1[:, 20:40], ok1, A.mult)
+        bar("v")
+        tt(T.ww[:, 0:20], T.w1[:, 0:20], ok2, A.mult)
+        tt(T.ww[:, 20:40], T.w1[:, 20:40], ok2, A.mult)
+        bar("v")
+        kzl = ts(T.zl[:], T.ww[:], 4.0, A.mult, T.cola[:, 3:4], A.add, tok())
+
+        win = T.th[:]
+        wait("a", kzl)
+        bar("a")
+        kgm = act(T.mz[:, 160:320], win.indirect(T.zl[:, 10:20]), sem=tok())
+        if t == 0:
+            wait("a", k6)
+            kfl = tok()
+            act(T.flg[:, 0:250:2], T.ii[:, 375:500], sem=kfl)
+            act(T.flg[:, 1:250:2], T.ii[:, 375:500], 1.0, 20.0, sem=kfl)
+            act(T.lift[:, 160:256], T.lift[:, 0:96], sem=kfl)
+            for ap, n in ((T.flg[:, 250:256], 6), (T.jj[:, 250:256], 6), (T.val[:, 250:256], 6), (T.fe[:, 40:48], 8)):
+                zero(ap, n, kfl)
+            khz = zero(T.hh[:, 0:800:2], 400, tok())
+        kt01 = tok()
+        for b in range(2):
+            act(T.t01[:, C * b:C * b + C], T["pd%d" % b][:, 0:C], sem=kt01)
+        bar("v")
+        wait("v", kth)
+        cp(T.mz[:, 0:160], win.indirect(T.zl[:, 0:10]))
+        bar("v")
+        wait("v", kgm)
+        tt(T.zt[:, 0:320], win.indirect(T.zl[:, 20:40]), T.mz[:], A.add)
+        bar("v")
+        kqz = quant(lq[:, K:K + 128], ls[:, K:K + 128], T.zt[:], tok())
+        wait("g", kqz)
+        send(lq[:, 0:K].bitcast(dt.uint8), lq[:, K:2 * K].bitcast(dt.uint8), "rc%d" % t, dst)
+        send(ls[:, 0:K], ls[:, K:2 * K], "rs%d" % t, dst)
+
+        if t == 0:
+            wait("v", k6)
+            ts(T.ge[:], T.ii[:, 0:125], qc, A.add, 20.0, A.is_ge)
+            bar("v")
+            tt(T.jj[:, 0:250:2], T.ge[:], T.ii[:, 125:250], A.add)
+            ts(T.gt[:], T.ge[:], -40.0, A.mult, T.cola[:, 4:5], A.add)
+            wait("v", kfl)
+            wrap(T.glo[:], T.flg[:], 256)
+            cp(T.jj[:, 1:250:2], T.jj[:, 0:250:2])
+            tt(T.val[:, 0:250:2], T.gt[:], T.ii[:, 250:375], A.add)
+            bar("v")
+            ts(T.val[:, 1:250:2], T.val[:, 0:250:2], -1.0, A.add)
+            ms(T.jj[:, 0:250:10], 1000.0)
+            ms(T.jj[:, 1:250:10], 1000.0)
+        if t == 1:
+            wait("v", dv, kfo)
+            kv = quant(T.qv[:], T.sv[:], T.vin[:], tok())
+            kol = wrap(T.olo[:], T.flo[:], 160, sem=tok())
+        if t == 2:
+            tt(T.o1[:, 0:20], az, nz, A.subtract)
+            tt(T.o1[:, 20:40], sz_, nz, A.add)
+            tt(ok, ok1, ok2, A.mult)
+            bar("v")
+            tt(T.o1[:, 40:60], T.o1[:, 0:20], sz_, A.max)
+            tt(T.o1[:, 60:80], T.o1[:, 20:40], az, A.min)
+            bar("v")
+            tt(T.o2[:, 0:20], T.o1[:, 40:60], ok, A.mult)
+            ts(T.o1[:, 80:100], T.o1[:, 60:80], -1.0, A.add)
+            bar("v")
+            tt(T.o2[:, 20:40], T.o1[:, 80:100], ok, A.mult)
+            bar("v")
+            wait("a", cp(T.oo[:], T.o2[:], tok()), kol)
+            act(T.orep[:], T.tab[:].indirect(T.oo[:]), 1.0, -1.0)
+            bar("a")
+            wait("y", act(T.obt[:], T.orep[:].indirect(T.olo[:]), sem=tok()))
+            dma("y", T.ob[:], T.obt[0:128:16, :])
+
+        ng, ag, sg = T["ng%d" % (t % 2)][:], lb[:, 41:80:2], lb[:, 1:40:2]
+        wait("v", "rn%d" % (t % 2), "rb%d" % t)
+        tt(T.f1[:, 0:20], ag, ng, A.subtract)
+        tt(T.f1[:, 20:40], sg, ng, A.add)
+        bar("v")
+        tt(T.fe[:, 0:20], T.f1[:, 0:20], sg, A.max)
+        tt(T.f1[:, 40:60], T.f1[:, 20:40], ag, A.min)
+        bar("v")
+        tt(T.fe[:, 20:40], T.f1[:, 40:60], T.fe[:, 0:20], A.max)
+        bar("v")
+        tt(T.nf[:], T.fe[:].indirect(T.glo[:]), T.jj[:], A.is_gt)
+        bar("v")
+        scan(T.gs[:], T.nf[:], T.val[:], A.mult, A.max)
+        bar("v")
+        kel = cp(T.el[:, 0:25], T.gs[:, 9:250:10], tok())
+
+        wait("p", dw, kqz, "rc%d" % t, "rs%d" % t)
+        kh = {}
+        for b in (0, 2, 1, 3):
+            kh[b] = mm(T["ph%d" % b][:, 0:128], T.qw[:, 128 * b:128 * b + 128], T.sw[:, 128 * b:128 * b + 128], lq[:, 0:128], ls[:, 0:128])
+        el = T.el[:, 0:25]
+        hw = [T.hh[:, 200 * b:200 * b + 200] for b in range(4)]
+        kh1 = tok()
+        for b in (2, 1, 3):
+            wait("a", kh[b])
+            act(T.hh[:, 200 * b + 1:200 * b + 160:2], T["ph%d" % b][:, 0:K], 0.03125, sem=kh1 if b == 1 else None)
+        wait("a", kel)
+        bar("a")
+        kg2 = act(T.g2[:], hw[2].indirect(el), sem=tok())
+        kg3 = act(T.g3[:], hw[3].indirect(el), sem=tok())
+        wait("v", kh[0])
+        ts(T.hh[:, 1:160:2], T.ph0[:, 0:K], 0.03125, A.mult)
+        bar("v")
+        wait("v", khz, kt01)
+        tt(T.xn[:, 0:1600:4], hw[0].indirect(el), T.t01[:, 0:C], A.add)
+        wait("v", kh1)
+        tt(T.xn[:, 1:1600:4], hw[1].indirect(el), T.t01[:, C:2 * C], A.add)
+        wait("v", kg2)
+        tt(T.xn[:, 2:1600:4], T.g2[:], T.pd2[:, 0:C], A.add)
+        wait("v", kg3)
+        tt(T.xn[:, 3:1600:4], T.g3[:], T.pd3[:, 0:C], A.add)
+        xs = T.xn
+
+    bar("v")
+    wait("p", kv)
+    kx, ky = [], []
+    for h in range(2):
+        q, s_ = T.qx[:, 200 * h:200 * h + 200], T.sx[:, 200 * h:200 * h + 200]
+        kx.append(quant(q, s_, xs[:, 800 * h:800 * h + 800], tok()))
+        wait("p", kx[h])
+        ky.append(mm(T["ph%d" % h][:, 0:200], T.qv[:], T.sv[:], q, s_))
+    wait("y", *kx)
+    dma("y", T.oc[:], T.qx[:].bitcast(dt.uint8))
+    for h in range(2):
+        wait("v", ky[h])
+        wait("y", cp(T.yt[:, 200 * h:200 * h + 200], T["ph%d" % h][:, 0:200], tok()))
+        dma("y", T.y[:, 200 * h:200 * h + 200], T.yt[:, 200 * h:200 * h + 200])
+    wait("a", *kx)
+    for k in range(4):
+        dma("a", T.osc[4 * k:4 * k + 4, :], T.sx[32 * k:32 * k + 4, :])
+    for s in list(total):
+        if max([seen.get((q, s), 0) for q in qs]) < total[s]:
+            wait("g", s)

@@ -13,8 +13,9 @@ for _d, _l in (
     (I32, "bli 8 pi 1 qi 3 upi 8"),
     (U16, "upo 8 blo 8 lno 10 nlo 40 plo 4 glo 16 olo 10 el 26 zl 40 oo 40"),
     (F32, "hh 800 g2 400 g3 400 yt 400 ex 400 qf 3 cola 8 colb 8 tab 32 t16 160 lift 256 il 10 xg 10 ln 10 a80 80 c640 640 hn 640 npk 40 "
-          "ns 80 n1 80 ta 80 d0a 240 c1 40 iz 20 iz2 40 flp 48 flg 256 flo 160 wsc 256 ii 500 ge 125 gt 125 jj 256 val 256 "
-          "nf 256 gs 256 cand 160 hs 160 aa 60 oa 61 bb 320 u0r 48 r1r 40 yy 80 x1 40 sm 60 fe 48 f1 60 w1 40 ww 40 o1 120 o2 40 orep 640 obt 160"),
+          "ns 80 n1 80 ta 80 n12 80 d0a 240 c1 40 iz 20 iz2 40 flp 48 flg 256 flo 160 wsc 256 ii 500 ge 125 gt 125 jj 256 val 256 "
+          "nf 256 gs 256 cand 160 hs 160 gk 80 pv 80 thr 80 v0 20 bb 300 u0r 48 r1r 40 yy 80 x1 40 sm 60 fe 48 f1 60 w1 40 ww 40 "
+          "o1 120 o2 40 orep 640 obt 160"),
 ):
     _w = _l.split()
     for _i in range(0, len(_w), 2):
@@ -22,7 +23,7 @@ for _d, _l in (
 for _b in range(4):
     SCRATCH["pd%d" % _b] = ("psum", [128, 512], F32)
     SCRATCH["ph%d" % _b] = ("psum", [128, 512], F32)
-SEMAPHORES = ["cv", "ca", "cg", "sent", "rn0", "rn1"] + ["r%s%d" % (n, t) for n in "bcs" for t in range(R)] + ["s%d" % i for i in range(128)]
+SEMAPHORES = ["cv", "cw", "ca", "cg", "sent", "rn0", "rn1"] + ["r%s%d" % (n, t) for n in "bcs" for t in range(R)] + ["s%d" % i for i in range(128)]
 
 
 def rank_program(g, core, T, topo):
@@ -32,6 +33,7 @@ def rank_program(g, core, T, topo):
     V, S, P, Y = g.vector, g.scalar, g.tensor, g.sync
     qs = {"v": V, "a": S, "p": P, "y": Y, "g": g}
     total, seen, pend, nxt = {}, {}, {"v": [], "a": [], "g": []}, [0]
+    W2 = ["cv", "cw"]
 
     def tok():
         nxt[0] += 1
@@ -118,6 +120,8 @@ def rank_program(g, core, T, topo):
     ko = ms(T.ones[:], 1.0, tok())
     ms(T.eb[:], 0.0, ko)
     ms(T.flp[:], 0.0, ko)
+    ms(T.reset[:], 0.0)
+    ms(T.ex[:, 0:400:200], BIG)
     wait("g", ko)
     op("g", g.affine_select(T.eb[:, 3:515:4], T.ones[:], [[1, 128]], A.is_equal, 0.0, 0, -1), k3)
     iota(T.flp[:, 0:40], [[-20, 4], [2, 10]], 60, k5)
@@ -129,64 +133,61 @@ def rank_program(g, core, T, topo):
     ts(T.qi[:, 1:2], T.pi[:], 2, A.logical_shift_right, 3, A.bitwise_and)
     ts(T.qi[:, 2:3], T.pi[:], 3, A.bitwise_and)
     kup = cp(T.upo[:], T.upi[:], tok())
-    bar("v")
+    wait("v", "cv")
     kq = cp(T.qf[:], T.qi[:], tok())
-    ms(T.reset[:], 0.0)
-    bar("v")
+    ms(T.reset[:, 0:200:20], BIG, "cw")
+    wait("v", kq)
     qc, rc, bc = T.qf[:, 0:1], T.qf[:, 1:2], T.qf[:, 2:3]
-    ts(T.ln[:, 0:10:2], T.il[:, 0:5], rc, A.add)
     ts(T.xg[:, 0:5], T.il[:, 5:10], qc, A.add)
-    ms(T.reset[:, 0:200:20], BIG)
+    ts(T.ln[:, 0:10:2], T.il[:, 0:5], rc, A.add, sem="cw")
+    wait("v", "cv")
+    ts(T.xg[:, 5:10], T.xg[:, 0:5], 20.0, A.is_ge, -20.0, A.mult)
     wait("v", k2)
     kt = ms(T.t16[:, 0:160:16], -1000.0, tok())
-    bar("v")
-    ts(T.xg[:, 5:10], T.xg[:, 0:5], 20.0, A.is_ge, -20.0, A.mult)
-    ms(T.ex[:, 0:400:200], BIG)
-    bar("v")
+    wait("v", "cv")
     tt(T.ln[:, 1:10:2], T.xg[:, 0:5], T.xg[:, 5:10], A.add)
-    wait("v", db)
-    kb = cp(T.blo[:, 0:5], T.bli[:, 0:5], tok())
     bar("v")
     knl = tok()
     for k in range(4):
         ts(T.nlo[:, 10 * k:10 * k + 10], T.ln[:], 4.0, A.mult, float(3 - k), A.add, knl)
+    wait("v", db)
+    kb = cp(T.blo[:, 0:5], T.bli[:, 0:5], tok())
     ts(T.lno[:], T.ln[:], 20.0, A.mult, 19.0, A.add)
     wait("v", k3)
     ke = tok()
     for b in range(4):
         quant(T.qe[:, 128 * b:128 * b + 128], T.se[:, 128 * b:128 * b + 128], T.eb[:, 3 - b:515 - b], ke)
-    wait("v", du)
-    kqu = quant(T.qu[:], T.su[:], T.uin[:], tok())
-    bar("v")
-    kpu = cp(T.qu2[:].bitcast(dt.uint32), T.qu[:].bitcast(dt.uint32).indirect(T.upo[:]), tok())
 
     wait("a", kq)
     kc = tok()
-    act(T.cola[:, 0:1], qc, -2048.0, -1024.0, sem=kc)
-    act(T.cola[:, 1:2], qc, -32.0, 480.0, F.Square, kc)
-    act(T.cola[:, 2:3], rc, 20.0, -1.0, sem=kc)
+    act(T.cola[:, 1:2], qc, -32.0, 480.0, F.Square)
+    act(T.cola[:, 2:3], rc, 20.0, -1.0)
+    act(T.cola[:, 0:1], qc, -2048.0, -1024.0)
     act(T.cola[:, 3:4], bc, 1.0, 1600.0, sem=kc)
     act(T.cola[:, 4:5], qc, 2.0, 0.0, sem=kc)
-    bar("a")
+    act(T.colb[:, 3:4], rc, 20.0, -2.0, sem=kc)
+    wait("a", "ca", kt)
+    act(T.lift[:, 0:160], T.t16[:], 2048.0, T.cola[:, 0:1], sem=kc)
     act(T.colb[:, 0:1], T.cola[:, 1:2], -1.0, 0.0, sem=kc)
     act(T.colb[:, 1:2], T.cola[:, 1:2], 1.0, 45.0, sem=kc)
     act(T.colb[:, 2:3], T.cola[:, 1:2], 1.0, 67.0, sem=kc)
-    act(T.colb[:, 3:4], T.cola[:, 2:3], 1.0, -1.0, sem=kc)
-    wait("a", kt)
-    act(T.lift[:, 0:160], T.t16[:], 2048.0, T.cola[:, 0:1], sem=kc)
     wait("a", k1, kb)
     act(T.a80[:], T.tab[:].indirect(T.blo[:, 0:5]))
     bar("a")
     wait("a", knl)
     kc6 = act(T.c640[:], T.a80[:].indirect(T.nlo[:]), sem=tok())
+    wait("v", du)
+    kqu = quant(T.qu[:], T.su[:], T.uin[:], tok())
+    wait("v", kc, k5)
+    wrap(T.plo[:, 0:3], T.flp[:], 48)
+    kpu = cp(T.qu2[:].bitcast(dt.uint32), T.qu[:].bitcast(dt.uint32).indirect(T.upo[:]), tok())
     wait("a", kup, kqu)
     ksu = op("a", S.activation(T.su2[:], T.su[:].indirect(T.upo[:]), F.Copy), tok())
     wait("a", k4)
-    kn = tok()
-    for ap, n in ((T.d0a[:, 0:240:3], 80), (T.d0a[:, 2:240:3], 80), (T.aa[:, 2:60:3], 20), (T.oa[:, 0:1], 1), (T.bb[:, 0:60:3], 20)):
-        zero(ap, n, kn)
-    wait("v", kc, k5)
-    wrap(T.plo[:, 0:3], T.flp[:], 48)
+    kn = zero(T.d0a[:, 0:240:3], 80, tok())
+
+    def halves(buf, n):
+        return [buf[:, n * h:n * h + n] for h in range(2)]
 
     xs = T.xin
     for t in range(R):
@@ -195,14 +196,11 @@ def rank_program(g, core, T, topo):
 
         if t == 0:
             wait("p", kpu, ksu)
-        else:
-            bar("v")
         ks, sb = [], [T.ph3, T.ph2]
         for h in range(2):
-            if t == 0:
-                wait("v", dx[h])
-            q, s_ = T.qx[:, 200 * h:200 * h + 200], T.sx[:, 200 * h:200 * h + 200]
-            wait("p", quant(q, s_, xs[:, 800 * h:800 * h + 800], tok()))
+            wait("v", dx[h] if t == 0 else W2[h])
+            q, s_ = halves(T.qx, 200)[h], halves(T.sx, 200)[h]
+            wait("p", quant(q, s_, halves(xs, 800)[h], tok()))
             ks.append(mm(sb[h][:, 0:200], T.qu2[:], T.su2[:], q, s_))
         if t == 0:
             wait("p", ke)
@@ -215,16 +213,17 @@ def rank_program(g, core, T, topo):
                 scan(T.hn[:, 160 * k:160 * k + 160], T.lift[:, 0:160], T.c640[:, 160 * k:160 * k + 160], A.add, A.max, sem=khn)
             wait("a", khn, k7)
             nfx = T.colb[:, 0:1]
-            act(T.npk[:], T.hn[:, 15:640:16], 1.0, nfx)
+            kng = act(T.n1g[:], T.hn[:, 31:640:32], 1.0, nfx, sem=tok())
             act(T.ns[:, 1:80:2], T.hn[:, 15:640:16], 1.0, nfx)
             for s in range(4):
                 act(T.ns[:, 20 * s:20 * s + 20:2], T.hn[:, 160 * (3 - s) + 15:160 * (4 - s):16], 1.0, nfx)
-            kng = act(T.n1g[:], T.hn[:, 31:640:32], 1.0, nfx, sem=tok())
-            bar("a")
+            kn2 = act(T.npk[:], T.hn[:, 15:640:16], 1.0, nfx, sem=tok())
+            wait("a", "ca")
             act(T.n1[:], T.ns[:], 1.0, 1.0, sem=kn)
             act(T.ta[:], T.ns[:], -1.0, 32.0, sem=kn)
+            act(T.n12[:], T.ns[:], 1.0, 12.0, sem=kn)
             act(T.d0a[:, 1:240:3], T.ns[:], 1.0, 34.0, sem=kn)
-            kn2 = act(T.iz2[:, 0:20], T.iz[:], 1.0, T.cola[:, 2:3], sem=tok())
+            act(T.iz2[:, 0:20], T.iz[:], 1.0, T.cola[:, 2:3], sem=kn2)
             act(T.iz2[:, 20:40], T.iz[:], 1.0, T.colb[:, 3:4], sem=kn2)
             iota(T.ii[:, 0:125], [[0, 5], [-4, 5], [0, 5]], 20, k6)
             iota(T.ii[:, 125:250], [[4, 5], [1, 5], [0, 5]], 0, k6)
@@ -234,7 +233,6 @@ def rank_program(g, core, T, topo):
             for j in range(2):
                 send(T["ng%d" % j][:], T.n1g[:], "rn%d" % j, T.cores[rank ^ STEP[j]])
             kfo = iota(T.flo[:], [[4, 20], [-80, 4], [320, 2]], 240, tok())
-        bar("a")
         kth = tok()
         for b in range(2):
             wait("a", kd[b])
@@ -242,18 +240,22 @@ def rank_program(g, core, T, topo):
 
         for h in range(2):
             wait("v", ks[h])
-            scan(T.ex[:, 200 * h + 1:200 * h + 200], sb[h][:, 0:199], T.reset[:, 1:200], A.min, A.add, BIG)
-        bar("v")
+            scan(T.ex[:, 200 * h + 1:200 * h + 200], sb[h][:, 0:199], T.reset[:, 1:200], A.min, A.add, BIG, W2[h])
         for h in range(2):
-            tt(T.nn[:, 200 * h:200 * h + 200], sb[h][:, 0:200], T.ex[:, 200 * h:200 * h + 200], A.is_ge)
+            wait("v", W2[h])
+            tt(halves(T.nn, 200)[h], sb[h][:, 0:200], halves(T.ex, 200)[h], A.is_ge, W2[h])
         if t == 0:
             wait("v", k4)
+        for h in range(2):
+            wait("v", W2[h])
+            scan(halves(T.vv, 200)[h], halves(T.nn, 200)[h], halves(T.key, 200)[h], A.mult, A.max, sem=W2[h])
         bar("v")
-        scan(T.vv[:], T.nn[:], T.key[:], A.mult, A.max)
-        bar("v")
-        cp(T.cand[:], T.vv[:].indirect(T.lno[:]))
-        bar("v")
-        khs = scan(T.hs[:], T.lift[:, 0:160], T.cand[:], A.add, A.max, sem=tok())
+        cp(T.cand[:, 0:64], T.vv[:].indirect(T.lno[:, 0:4]))
+        cp(T.cand[:, 64:160], T.vv[:].indirect(T.lno[:, 4:10]), "cw")
+        wait("v", "cv")
+        khs = scan(T.hs[:, 0:64], T.lift[:, 0:64], T.cand[:, 0:64], A.add, A.max, sem=tok())
+        wait("v", "cw")
+        scan(T.hs[:, 64:160], T.lift[:, 0:96], T.cand[:, 64:160], A.add, A.max, sem=khs)
         bar("v")
         hs = T.hs[:, 15:160:16]
         ts(T.bb[:, 2:60:6], hs, T.cola[:, 1:2], A.subtract)
@@ -272,26 +274,56 @@ def rank_program(g, core, T, topo):
             wait("a", kd[b])
             act(T.th[:, b:1600:4], T["pd%d" % b][:, 0:C], 0.5, sem=kth)
 
+        def part(buf, s):
+            return buf[:, 20 * s:20 * s + 20]
+        u0 = T.bb[:, 2:60:3]
+
+        def fits(s):
+            tt(part(T.gk, s), u0, part(T.n12, s), A.is_gt, "cw" if s else None)
+
+        def times(s):
+            tt(part(T.pv, s), part(T.gk, s), T.v0[:], A.mult, "cw")
+
+        def limit(s):
+            tt(part(T.thr, s), part(T.pv, s), part(T.ta, s), A.add, "cw")
         for s in range(4):
-            bar("v")
-            u = T.bb[:, 60 * s + 2:60 * s + 60:3]
-            tt(T.aa[:, 1:60:3], u, T.n1[:, 20 * s:20 * s + 20], A.add)
-            tt(T.aa[:, 0:60:3], u, T.ta[:, 20 * s:20 * s + 20], A.is_gt)
+            wait("v", "cv")
+            u, z = T.bb[:, 60 * s + 2:60 * s + 60:3], T.d0a[:, 60 * s + 2:60 * s + 60:3]
+            tt(T.bb[:, 60 * s:60 * s + 60:3], u, part(T.ta, s), A.is_gt)
             if s == 0:
-                ts(T.bb[:, 300:320], u, 21.0, A.add)
-            bar("v")
-            scan(T.oa[:, 1:61], T.d0a[:, 60 * s:60 * s + 60], T.aa[:], A.mult, A.max)
-            bar("v")
-            tt(T.bb[:, 60 * s + 1:60 * s + 60:3], T.oa[:, 2:61:3], T.bb[:, 300:320], A.is_le)
-            bar("v")
-            scan(T.bb[:, 60 * s + 60:60 * s + 120], T.oa[:, 0:60], T.bb[:, 60 * s:60 * s + 60], A.mult, A.max)
+                fits(0)
+                tt(T.bb[:, 1:60:3], u, part(T.n1, 0), A.add, "cw")
+                ts(T.v0[:], u0, -12.0, A.add, sem="cw")
+                fits(1)
+                wait("v", "cv")
+                tt(z, part(T.gk, 0), T.bb[:, 0:60:3], A.is_ge)
+                wait("v", "cw")
+                times(1)
+                fits(2)
+            else:
+                tt(T.bb[:, 60 * s + 1:60 * s + 60:3], u, part(T.n1, s), A.add)
+                wait("v", "cw")
+                tt(z, u, part(T.thr, s), A.is_le)
+                if s == 1:
+                    limit(2)
+                    times(3)
+                if s == 3 and t == 0:
+                    wait("v", kn2)
+                    tt(T.c1[:, 0:20], T.iz2[:, 0:20], T.npk[:, 0:40:2], A.subtract, "cw")
+                    tt(T.c1[:, 20:40], T.iz2[:, 20:40], T.npk[:, 0:40:2], A.add, "cw")
+            wait("v", "cv")
+            scan(T.bb[:, 60 * s + 60:60 * s + 120], T.d0a[:, 60 * s:60 * s + 60], T.bb[:, 60 * s:60 * s + 60], A.mult, A.max)
+            if s < 2:
+                wait("v", "cw")
+            if s == 0:
+                limit(1)
+                times(2)
+                fits(3)
+            if s == 1:
+                limit(3)
         bar("v")
-        tt(T.yy[:], T.bb[:, 62:300:3], T.bb[:, 1:240:3], A.mult)
+        tt(T.yy[:], T.bb[:, 62:300:3], T.d0a[:, 2:240:3], A.mult)
         nz = T.npk[:, 0:40:2]
-        if t == 0:
-            wait("v", kn2)
-            tt(T.c1[:, 0:20], T.iz2[:, 0:20], nz, A.subtract)
-            tt(T.c1[:, 20:40], T.iz2[:, 20:40], nz, A.add)
         bar("v")
         wait("v", krp)
         ksn = tok()
@@ -303,20 +335,23 @@ def rank_program(g, core, T, topo):
         az, sz_, ok1, ok2, ok = ab[:, 40:80:2], ab[:, 0:40:2], T.sm[:, 0:20], T.sm[:, 20:40], T.sm[:, 40:60]
         tt(T.x1[:, 0:20], az, T.c1[:, 0:20], A.add)
         tt(T.x1[:, 20:40], sz_, T.c1[:, 20:40], A.add)
-        tt(ok1, az, sz_, A.is_gt)
-        bar("v")
+        tt(ok1, az, sz_, A.is_gt, "cw")
+        wait("v", "cv")
         tt(ok2, T.x1[:, 0:20], T.x1[:, 20:40], A.is_le)
+        wait("v", "cw")
         tt(T.w1[:, 0:20], T.x1[:, 0:20], ok1, A.mult)
-        tt(T.w1[:, 20:40], T.x1[:, 20:40], ok1, A.mult)
-        bar("v")
+        tt(T.w1[:, 20:40], T.x1[:, 20:40], ok1, A.mult, "cw")
+        wait("v", "cv")
         tt(T.ww[:, 0:20], T.w1[:, 0:20], ok2, A.mult)
-        tt(T.ww[:, 20:40], T.w1[:, 20:40], ok2, A.mult)
-        bar("v")
-        kzl = ts(T.zl[:], T.ww[:], 4.0, A.mult, T.cola[:, 3:4], A.add, tok())
+        wait("v", "cw")
+        tt(T.ww[:, 20:40], T.w1[:, 20:40], ok2, A.mult, "cw")
+        wait("v", "cv")
+        kzl = ts(T.zl[:, 0:20], T.ww[:, 0:20], 4.0, A.mult, T.cola[:, 3:4], A.add, tok())
+        wait("v", "cw")
+        ts(T.zl[:, 20:40], T.ww[:, 20:40], 4.0, A.mult, T.cola[:, 3:4], A.add, "cw")
 
         win = T.th[:]
-        wait("a", kzl)
-        bar("a")
+        wait("a", kzl, kth)
         kgm = act(T.mz[:, 160:320], win.indirect(T.zl[:, 10:20]), sem=tok())
         if t == 0:
             wait("a", k6)
@@ -330,12 +365,12 @@ def rank_program(g, core, T, topo):
         kt01 = tok()
         for b in range(2):
             act(T.t01[:, C * b:C * b + C], T["pd%d" % b][:, 0:C], sem=kt01)
-        bar("v")
-        wait("v", kth)
+        wait("v", kzl, kth)
         cp(T.mz[:, 0:160], win.indirect(T.zl[:, 0:10]))
         bar("v")
+        tt(T.zt[:, 0:160], win.indirect(T.zl[:, 20:30]), T.mz[:, 0:160], A.add)
         wait("v", kgm)
-        tt(T.zt[:, 0:320], win.indirect(T.zl[:, 20:40]), T.mz[:], A.add)
+        tt(T.zt[:, 160:320], win.indirect(T.zl[:, 30:40]), T.mz[:, 160:320], A.add)
         bar("v")
         kqz = quant(lq[:, K:K + 128], ls[:, K:K + 128], T.zt[:], tok())
         wait("g", kqz)
@@ -401,44 +436,48 @@ def rank_program(g, core, T, topo):
             kh[b] = mm(T["ph%d" % b][:, 0:128], T.qw[:, 128 * b:128 * b + 128], T.sw[:, 128 * b:128 * b + 128], lq[:, 0:128], ls[:, 0:128])
         el = T.el[:, 0:25]
         hw = [T.hh[:, 200 * b:200 * b + 200] for b in range(4)]
-        kh1 = tok()
-        for b in (2, 1, 3):
-            wait("a", kh[b])
-            act(T.hh[:, 200 * b + 1:200 * b + 160:2], T["ph%d" % b][:, 0:K], 0.03125, sem=kh1 if b == 1 else None)
-        wait("a", kel)
         bar("a")
+        wait("a", kh[2])
+        act(T.hh[:, 401:560:2], T.ph2[:, 0:K], 0.03125)
+        wait("a", kh[3])
+        kh3 = act(T.hh[:, 601:760:2], T.ph3[:, 0:K], 0.03125, sem=tok())
+        wait("a", kel, "ca")
         kg2 = act(T.g2[:], hw[2].indirect(el), sem=tok())
+        wait("a", kh3)
         kg3 = act(T.g3[:], hw[3].indirect(el), sem=tok())
-        wait("v", kh[0])
-        ts(T.hh[:, 1:160:2], T.ph0[:, 0:K], 0.03125, A.mult)
         bar("v")
+        for b in range(2):
+            wait("v", kh[b])
+            ts(T.hh[:, 200 * b + 1:200 * b + 160:2], T["ph%d" % b][:, 0:K], 0.03125, A.mult, sem=W2[b])
         wait("v", khz, kt01)
-        tt(T.xn[:, 0:1600:4], hw[0].indirect(el), T.t01[:, 0:C], A.add)
-        wait("v", kh1)
-        tt(T.xn[:, 1:1600:4], hw[1].indirect(el), T.t01[:, C:2 * C], A.add)
+        for b in range(2):
+            wait("v", W2[b])
+            tt(T.xn[:, b:1600:4], hw[b].indirect(el), T.t01[:, C * b:C * b + C], A.add)
         wait("v", kg2)
         tt(T.xn[:, 2:1600:4], T.g2[:], T.pd2[:, 0:C], A.add)
         wait("v", kg3)
-        tt(T.xn[:, 3:1600:4], T.g3[:], T.pd3[:, 0:C], A.add)
+        for h in range(2):
+            tt(T.xn[:, 800 * h + 3:800 * h + 800:4], halves(T.g3, 200)[h], T.pd3[:, 200 * h:200 * h + 200], A.add, W2[h])
         xs = T.xn
 
-    bar("v")
     wait("p", kv)
     kx, ky = [], []
     for h in range(2):
-        q, s_ = T.qx[:, 200 * h:200 * h + 200], T.sx[:, 200 * h:200 * h + 200]
-        kx.append(quant(q, s_, xs[:, 800 * h:800 * h + 800], tok()))
+        wait("v", W2[h])
+        q, s_ = halves(T.qx, 200)[h], halves(T.sx, 200)[h]
+        kx.append(quant(q, s_, halves(xs, 800)[h], tok()))
         wait("p", kx[h])
         ky.append(mm(T["ph%d" % h][:, 0:200], T.qv[:], T.sv[:], q, s_))
     wait("y", *kx)
     dma("y", T.oc[:], T.qx[:].bitcast(dt.uint8))
-    for h in range(2):
-        wait("v", ky[h])
-        wait("y", cp(T.yt[:, 200 * h:200 * h + 200], T["ph%d" % h][:, 0:200], tok()))
-        dma("y", T.y[:, 200 * h:200 * h + 200], T.yt[:, 200 * h:200 * h + 200])
-    wait("a", *kx)
+    wait("v", ky[0])
+    wait("y", cp(T.yt[:, 0:200], T.ph0[:, 0:200], tok()))
+    dma("y", T.y[:, 0:200], T.yt[:, 0:200])
+    wait("v", ky[1])
+    wait("a", cp(T.yt[:, 200:400], T.ph1[:, 0:200], tok()))
+    dma("a", T.y[:, 200:400], T.yt[:, 200:400])
     for k in range(4):
-        dma("a", T.osc[4 * k:4 * k + 4, :], T.sx[32 * k:32 * k + 4, :])
+        dma("a" if k % 2 else "y", T.osc[4 * k:4 * k + 4, :], T.sx[32 * k:32 * k + 4, :])
     for s in list(total):
         if max([seen.get((q, s), 0) for q in qs]) < total[s]:
             wait("g", s)

@@ -3,6 +3,8 @@ from concourse.mybir import dt, AluOpType as A, ActivationFunctionType as F
 C, K, R = 400, 80, 3
 STEP = [1, 2, 1]
 BIG = 1e29
+CUT = [(0, 200), (200, 400)]
+END = [(0, 272), (272, 400)]
 Q4, U8, BF, F32, I32, U16 = "float8_e4m3fn_x4", "uint8", "bfloat16", "float32", "int32", "uint16"
 SCRATCH = {}
 for _d, _l in (
@@ -13,8 +15,8 @@ for _d, _l in (
     (I32, "bli 8 pi 1 qi 3 upi 8"),
     (U16, "upo 8 blo 8 lno 10 nlo 40 plo 4 glo 16 olo 10 el 26 zl 40 oo 40"),
     (F32, "hh 800 g2 400 g3 400 yt 400 ex 400 qf 3 cola 8 colb 8 tab 32 t16 160 lift 256 il 10 xg 10 ln 10 a80 80 c640 640 hn 640 npk 40 "
-          "ns 80 n1 80 ta 80 n12 80 d0a 240 c1 40 iz 20 iz2 40 flp 48 flg 256 flo 160 wsc 256 ii 500 ge 125 gt 125 jj 256 val 256 "
-          "nf 256 gs 256 cand 160 hs 160 gk 80 pv 80 thr 80 v0 20 bb 300 u0r 48 r1r 40 yy 80 x1 40 sm 60 fe 48 f1 60 w1 40 ww 40 "
+          "ns 80 n1 80 ta 80 n12 80 st 40 d0a 240 c1 40 iz 20 iz2 40 flp 48 flg 256 flo 160 wsc 256 ii 500 sg 125 ge 125 gt 125 jj 256 val 256 "
+          "nf 256 gs 256 cand 160 hs 160 gk 80 pv 80 thr 80 v0 20 bb 240 b3 60 yb 240 u0r 48 r1r 40 x1 40 sm 60 fe 48 f1 60 w1 40 ww 40 "
           "o1 120 o2 40 orep 640 obt 160"),
 ):
     _w = _l.split()
@@ -23,7 +25,7 @@ for _d, _l in (
 for _b in range(4):
     SCRATCH["pd%d" % _b] = ("psum", [128, 512], F32)
     SCRATCH["ph%d" % _b] = ("psum", [128, 512], F32)
-SEMAPHORES = ["cv", "cw", "ca", "cg", "sent", "rn0", "rn1"] + ["r%s%d" % (n, t) for n in "bcs" for t in range(R)] + ["s%d" % i for i in range(128)]
+SEMAPHORES = ["cv", "cw", "cx", "cy", "ca", "sent", "rn0", "rn1"] + ["r%s%d" % (n, t) for n in "bcs" for t in range(R)] + ["s%d" % i for i in range(133)]
 
 
 def rank_program(g, core, T, topo):
@@ -37,7 +39,7 @@ def rank_program(g, core, T, topo):
 
     def tok():
         nxt[0] += 1
-        return "s%d" % (nxt[0] - 1)
+        return SEMAPHORES[16 + nxt[0]]
 
     def op(q, ins, sem=None, n=1):
         sem = sem or "c" + q
@@ -98,19 +100,14 @@ def rank_program(g, core, T, topo):
         total["sent"] = total.get("sent", 0) + len(topo.engines(core, dst))
         total[sem] = len(topo.engines(dst, core))
 
-    def wrap(out, full, n, sem=None):
-        scan(T.wsc[:, 0:n], T.lift[:, 0:n], full, A.add, A.max)
-        bar("v")
-        return ts(out, T.wsc[:, 15:n:16], T.cola[:, 1:2], A.subtract, sem=sem)
-
     db = dma("a", T.bli[:, 0:5], T.bl[:])
     du = dma("a", T.uin[:], T.u[:])
-    dx = [dma("y", T.xin[:, 800 * h:800 * h + 800], T.x[:, 800 * h:800 * h + 800]) for h in range(2)]
+    dx = [dma("y", T.xin[:, 4 * a:4 * b], T.x[:, 4 * a:4 * b]) for a, b in CUT]
     dw = dma("y", T.qw[:].bitcast(dt.uint8), T.wc[:])
     dma("y", T.sw[:], T.ws[:], dw)
-    dv = dma("y", T.vin[:], T.v[:])
+    dma("y", T.vin[:], T.v[:], dw)
 
-    k0, k1, k2, k3, k4, k5, k6, k7 = [tok() for _ in range(8)]
+    k0, k1, k2, k3, k4, k5, k6 = [tok() for _ in range(7)]
     iota(T.pi[:], [[0, 1]], 0, k0, ch=1, whole=True)
     iota(T.upi[:], [[16, 8]], 0, k0, whole=True)
     iota(T.il[:, 0:5], [[4, 5]], 0, k0)
@@ -122,11 +119,13 @@ def rank_program(g, core, T, topo):
     ms(T.flp[:], 0.0, ko)
     ms(T.reset[:], 0.0)
     ms(T.ex[:, 0:400:200], BIG)
+    ms(T.b3[:], 0.0)
+    ms(T.yb[:], 0.0)
     wait("g", ko)
     op("g", g.affine_select(T.eb[:, 3:515:4], T.ones[:], [[1, 128]], A.is_equal, 0.0, 0, -1), k3)
-    iota(T.flp[:, 0:40], [[-20, 4], [2, 10]], 60, k5)
+    iota(T.flp[:, 0:40], [[-60, 4], [6, 10]], 182, k5)
+    iota(T.iz[:], [[0, 4], [80, 5]], -400, k5)
     iota(T.key[:], [[0, 20], [-1, 20]], 32, k4)
-    iota(T.iz[:], [[0, 4], [80, 5]], -400, k7)
 
     wait("v", k0)
     ts(T.qi[:, 0:1], T.pi[:], 15, A.bitwise_and)
@@ -146,120 +145,133 @@ def rank_program(g, core, T, topo):
     kt = ms(T.t16[:, 0:160:16], -1000.0, tok())
     wait("v", "cv")
     tt(T.ln[:, 1:10:2], T.xg[:, 0:5], T.xg[:, 5:10], A.add)
-    bar("v")
+    wait("v", db)
+    kb = cp(T.blo[:, 0:5], T.bli[:, 0:5], tok())
+    wait("v", "cv", "cw")
     knl = tok()
     for k in range(4):
         ts(T.nlo[:, 10 * k:10 * k + 10], T.ln[:], 4.0, A.mult, float(3 - k), A.add, knl)
-    wait("v", db)
-    kb = cp(T.blo[:, 0:5], T.bli[:, 0:5], tok())
     ts(T.lno[:], T.ln[:], 20.0, A.mult, 19.0, A.add)
+    wait("v", du)
+    kqu = quant(T.qu[:], T.su[:], T.uin[:], tok())
     wait("v", k3)
     ke = tok()
-    for b in range(4):
+    for b in range(2):
         quant(T.qe[:, 128 * b:128 * b + 128], T.se[:, 128 * b:128 * b + 128], T.eb[:, 3 - b:515 - b], ke)
+    wait("v", kqu, kup)
+    kpu = cp(T.qu2[:].bitcast(dt.uint32), T.qu[:].bitcast(dt.uint32).indirect(T.upo[:]), tok())
 
     wait("a", kq)
     kc = tok()
     act(T.cola[:, 1:2], qc, -32.0, 480.0, F.Square)
-    act(T.cola[:, 2:3], rc, 20.0, -1.0)
     act(T.cola[:, 0:1], qc, -2048.0, -1024.0)
+    act(T.cola[:, 2:3], rc, 20.0, -1.0, sem=kc)
     act(T.cola[:, 3:4], bc, 1.0, 1600.0, sem=kc)
     act(T.cola[:, 4:5], qc, 2.0, 0.0, sem=kc)
     act(T.colb[:, 3:4], rc, 20.0, -2.0, sem=kc)
+    act(T.cola[:, 5:6], qc, 1.0, -19.5, sem=kc)
     wait("a", "ca", kt)
+    fix = T.cola[:, 1:2]
     act(T.lift[:, 0:160], T.t16[:], 2048.0, T.cola[:, 0:1], sem=kc)
-    act(T.colb[:, 0:1], T.cola[:, 1:2], -1.0, 0.0, sem=kc)
-    act(T.colb[:, 1:2], T.cola[:, 1:2], 1.0, 45.0, sem=kc)
-    act(T.colb[:, 2:3], T.cola[:, 1:2], 1.0, 67.0, sem=kc)
+    for j, sc, bi in ((0, -1.0, 0.0), (1, 1.0, 45.0)):
+        act(T.colb[:, j:j + 1], fix, sc, bi, sem=kc)
     wait("a", k1, kb)
     act(T.a80[:], T.tab[:].indirect(T.blo[:, 0:5]))
-    bar("a")
-    wait("a", knl)
-    kc6 = act(T.c640[:], T.a80[:].indirect(T.nlo[:]), sem=tok())
-    wait("v", du)
-    kqu = quant(T.qu[:], T.su[:], T.uin[:], tok())
-    wait("v", kc, k5)
-    wrap(T.plo[:, 0:3], T.flp[:], 48)
-    kpu = cp(T.qu2[:].bitcast(dt.uint32), T.qu[:].bitcast(dt.uint32).indirect(T.upo[:]), tok())
+    for j, bi in ((2, 67.0), (4, 32.0), (5, 13.0), (6, 12.0), (7, 33.0)):
+        act(T.colb[:, j:j + 1], fix, 1.0, bi, sem=kc)
     wait("a", kup, kqu)
-    ksu = op("a", S.activation(T.su2[:], T.su[:].indirect(T.upo[:]), F.Copy), tok())
+    op("a", S.activation(T.su2[:], T.su[:].indirect(T.upo[:]), F.Copy), kpu)
+    wait("a", "ca", knl)
+    kc6 = act(T.c640[:], T.a80[:].indirect(T.nlo[:]), sem=tok())
     wait("a", k4)
     kn = zero(T.d0a[:, 0:240:3], 80, tok())
 
-    def halves(buf, n):
-        return [buf[:, n * h:n * h + n] for h in range(2)]
-
     xs = T.xin
+    sb = [T.ph3, T.ph2]
+
+    def scores(h, cut, src, side, sc):
+        a, b = cut[h]
+        k = quant(T.qx[:, a:b], T.sx[:, a:b], src[:, 4 * a:4 * b], tok())
+        wait("p", k)
+        return k, mm(sb[h][:, 0:b - a], side[:], sc[:], T.qx[:, a:b], T.sx[:, a:b])
+
     for t in range(R):
         dst = T.cores[rank ^ STEP[t]]
         lq, ls, lb, ab = [T["%s%d" % (n, t)] for n in ("lq", "ls", "lb", "snd")]
 
         if t == 0:
-            wait("p", kpu, ksu)
-        ks, sb = [], [T.ph3, T.ph2]
+            wait("p", kpu)
+        ks = []
         for h in range(2):
             wait("v", dx[h] if t == 0 else W2[h])
-            q, s_ = halves(T.qx, 200)[h], halves(T.sx, 200)[h]
-            wait("p", quant(q, s_, halves(xs, 800)[h], tok()))
-            ks.append(mm(sb[h][:, 0:200], T.qu2[:], T.su2[:], q, s_))
+            ks.append(scores(h, CUT, xs, T.qu2, T.su2)[1])
         if t == 0:
+            for b in range(2, 4):
+                quant(T.qe[:, 128 * b:128 * b + 128], T.se[:, 128 * b:128 * b + 128], T.eb[:, 3 - b:515 - b], ke)
             wait("p", ke)
+            wait("v", "cv", "cw")
         kd = [mm(T["pd%d" % b][:, 0:C], T.qe[:, 128 * b:128 * b + 128], T.se[:, 128 * b:128 * b + 128], T.qx[:], T.sx[:]) for b in range(4)]
 
+        for h, (a, b) in enumerate(CUT):
+            wait("v", ks[h])
+            scan(T.ex[:, a + 1:b], sb[h][:, 0:b - a - 1], T.reset[:, 1:b - a], A.min, A.add, BIG, W2[h])
         if t == 0:
-            wait("v", kc6)
+            wait("v", kc6, kc)
             khn = tok()
             for k in range(4):
                 scan(T.hn[:, 160 * k:160 * k + 160], T.lift[:, 0:160], T.c640[:, 160 * k:160 * k + 160], A.add, A.max, sem=khn)
-            wait("a", khn, k7)
+            wait("a", khn, k5, kc)
             nfx = T.colb[:, 0:1]
-            kng = act(T.n1g[:], T.hn[:, 31:640:32], 1.0, nfx, sem=tok())
             act(T.ns[:, 1:80:2], T.hn[:, 15:640:16], 1.0, nfx)
             for s in range(4):
                 act(T.ns[:, 20 * s:20 * s + 20:2], T.hn[:, 160 * (3 - s) + 15:160 * (4 - s):16], 1.0, nfx)
+            kng = act(T.n1g[:], T.hn[:, 31:640:32], 1.0, nfx, sem=tok())
             kn2 = act(T.npk[:], T.hn[:, 15:640:16], 1.0, nfx, sem=tok())
             wait("a", "ca")
-            act(T.n1[:], T.ns[:], 1.0, 1.0, sem=kn)
-            act(T.ta[:], T.ns[:], -1.0, 32.0, sem=kn)
+            nl, nr = T.ns[:, 0:20:2], T.ns[:, 1:20:2]
+            kst = tok()
+            for j, (src, sc, col) in enumerate([(nl, -1.0, 4), (nr, 1.0, 5), (nl, 1.0, 6), (nr, -1.0, 7)]):
+                act(T.st[:, 10 * j:10 * j + 10], src, sc, T.colb[:, col:col + 1], sem=kst)
             act(T.n12[:], T.ns[:], 1.0, 12.0, sem=kn)
+            act(T.n1[:], T.ns[:], 1.0, 1.0, sem=kn)
             act(T.d0a[:, 1:240:3], T.ns[:], 1.0, 34.0, sem=kn)
+            act(T.ta[:], T.ns[:], -1.0, 32.0, sem=kn)
             act(T.iz2[:, 0:20], T.iz[:], 1.0, T.cola[:, 2:3], sem=kn2)
             act(T.iz2[:, 20:40], T.iz[:], 1.0, T.colb[:, 3:4], sem=kn2)
             iota(T.ii[:, 0:125], [[0, 5], [-4, 5], [0, 5]], 20, k6)
             iota(T.ii[:, 125:250], [[4, 5], [1, 5], [0, 5]], 0, k6)
-            iota(T.ii[:, 250:375], [[0, 5], [-8, 5], [-40, 5]], 201, k6)
+            iota(T.ii[:, 250:375], [[0, 5], [-8, 5], [-40, 5]], 181, k6)
             iota(T.ii[:, 375:500], [[0, 5], [1, 5], [-5, 5]], 20, k6)
             wait("g", kng)
             for j in range(2):
                 send(T["ng%d" % j][:], T.n1g[:], "rn%d" % j, T.cores[rank ^ STEP[j]])
             kfo = iota(T.flo[:], [[4, 20], [-80, 4], [320, 2]], 240, tok())
         kth = tok()
-        for b in range(2):
-            wait("a", kd[b])
-            act(T.th[:, b:1600:4], T["pd%d" % b][:, 0:C], 0.5, sem=kth)
-
-        for h in range(2):
-            wait("v", ks[h])
-            scan(T.ex[:, 200 * h + 1:200 * h + 200], sb[h][:, 0:199], T.reset[:, 1:200], A.min, A.add, BIG, W2[h])
-        for h in range(2):
+        if t:
+            for b in range(2):
+                wait("a", kd[b])
+                act(T.th[:, b:1600:4], T["pd%d" % b][:, 0:C], 0.5, sem=kth)
+        for h, (a, b) in enumerate(CUT):
             wait("v", W2[h])
-            tt(halves(T.nn, 200)[h], sb[h][:, 0:200], halves(T.ex, 200)[h], A.is_ge, W2[h])
+            tt(T.nn[:, a:b], sb[h][:, 0:b - a], T.ex[:, a:b], A.is_ge, W2[h])
         if t == 0:
-            wait("v", k4)
-        for h in range(2):
+            wait("v", k4, k5)
+        for h, (a, b) in enumerate(CUT):
             wait("v", W2[h])
-            scan(halves(T.vv, 200)[h], halves(T.nn, 200)[h], halves(T.key, 200)[h], A.mult, A.max, sem=W2[h])
-        bar("v")
-        cp(T.cand[:, 0:64], T.vv[:].indirect(T.lno[:, 0:4]))
-        cp(T.cand[:, 64:160], T.vv[:].indirect(T.lno[:, 4:10]), "cw")
+            scan(T.vv[:, a:b], T.nn[:, a:b], T.key[:, a:b], A.mult, A.max, sem=W2[h])
+        if t == 0:
+            scan(T.wsc[:, 0:48], T.lift[:, 0:48], T.flp[:], A.add, A.max, sem="cx")
+        wait("v", "cv", "cw")
+        cp(T.cand[:, 0:96], T.vv[:].indirect(T.lno[:, 0:6]))
+        cp(T.cand[:, 96:160], T.vv[:].indirect(T.lno[:, 6:10]), "cw")
         wait("v", "cv")
-        khs = scan(T.hs[:, 0:64], T.lift[:, 0:64], T.cand[:, 0:64], A.add, A.max, sem=tok())
+        khs = scan(T.hs[:, 0:96], T.lift[:, 0:96], T.cand[:, 0:96], A.add, A.max, sem=tok())
         wait("v", "cw")
-        scan(T.hs[:, 64:160], T.lift[:, 0:96], T.cand[:, 64:160], A.add, A.max, sem=khs)
-        bar("v")
+        scan(T.hs[:, 96:160], T.lift[:, 0:64], T.cand[:, 96:160], A.add, A.max, sem=khs)
+        if t == 0:
+            wait("v", "cx")
+            ts(T.plo[:, 0:3], T.wsc[:, 15:48:16], fix, A.subtract, sem="cx")
         hs = T.hs[:, 15:160:16]
-        ts(T.bb[:, 2:60:6], hs, T.cola[:, 1:2], A.subtract)
-        ts(T.bb[:, 5:60:6], hs, -1.0, A.mult, T.colb[:, 1:2], A.add)
         wait("a", khs)
         krp = tok()
         for k in range(4):
@@ -267,10 +279,19 @@ def rank_program(g, core, T, topo):
             act(T.r1r[:, 10 * k:10 * k + 10], hs, -1.0, T.colb[:, 2:3], sem=krp)
         if t == 0:
             zero(T.u0r[:, 40:48], 8, krp)
+            wait("a", k6)
+            kfl = tok()
+            act(T.sg[:], T.ii[:, 0:125], 1.0, T.cola[:, 5:6], F.Sign)
+            act(T.flg[:, 0:250:2], T.ii[:, 375:500], sem=kfl)
+            act(T.flg[:, 1:250:2], T.ii[:, 375:500], 1.0, 20.0, sem=kfl)
+            act(T.lift[:, 160:256], T.lift[:, 0:96], sem=kfl)
+            zero(T.flg[:, 250:256], 6, kfl)
+            wait("a", "ca")
+            act(T.ge[:], T.sg[:], 0.5, 0.5, sem=kfl)
+            act(T.gt[:], T.sg[:], -20.0, T.cola[:, 4:5], sem=kfl)
             zero(T.th[:, 1600:1616], 16, kth)
             zero(T.zt[:, 320:512], 192, kth)
-            wait("v", kn)
-        for b in range(2, 4):
+        for b in range(2 if t else 0, 4):
             wait("a", kd[b])
             act(T.th[:, b:1600:4], T["pd%d" % b][:, 0:C], 0.5, sem=kth)
 
@@ -278,60 +299,76 @@ def rank_program(g, core, T, topo):
             return buf[:, 20 * s:20 * s + 20]
         u0 = T.bb[:, 2:60:3]
 
-        def fits(s):
-            tt(part(T.gk, s), u0, part(T.n12, s), A.is_gt, "cw" if s else None)
+        def fits(s, sem):
+            tt(part(T.gk, s), u0, part(T.n12, s), A.is_gt, sem)
 
-        def times(s):
-            tt(part(T.pv, s), part(T.gk, s), T.v0[:], A.mult, "cw")
+        def times(s, sem):
+            tt(part(T.pv, s), part(T.gk, s), T.v0[:], A.mult, sem)
 
-        def limit(s):
-            tt(part(T.thr, s), part(T.pv, s), part(T.ta, s), A.add, "cw")
-        for s in range(4):
+        def limit(s, sem):
+            tt(part(T.thr, s), part(T.pv, s), part(T.ta, s), A.add, sem)
+        wait("v", khs)
+        if t == 0:
+            wait("v", kst)
+        st = [T.st[:, 10 * j:10 * j + 10] for j in range(4)]
+        ts(T.bb[:, 2:60:6], hs, fix, A.subtract, sem="cw")
+        ts(T.bb[:, 5:60:6], hs, -1.0, A.mult, T.colb[:, 1:2], A.add, "cw")
+        tt(T.bb[:, 0:60:6], hs, st[0], A.is_gt)
+        tt(T.bb[:, 3:60:6], hs, st[1], A.is_lt)
+        tt(T.gk[:, 0:20:2], hs, st[2], A.is_gt)
+        tt(T.gk[:, 1:20:2], hs, st[3], A.is_lt)
+        wait("v", "cw")
+        if t == 0:
+            wait("v", kn)
+        fits(1, "cw")
+        ts(T.v0[:], u0, -12.0, A.add, sem="cw")
+        tt(T.bb[:, 1:60:3], u0, part(T.n1, 0), A.add, "cy")
+        wait("v", "cv")
+        tt(T.d0a[:, 2:60:3], part(T.gk, 0), T.bb[:, 0:60:3], A.is_ge)
+        fits(2, "cy")
+        wait("v", "cw")
+        times(1, "cx")
+        fits(3, "cw")
+        wait("v", "cv", "cy")
+        scan(T.bb[:, 60:120], T.d0a[:, 0:60], T.bb[:, 0:60], A.mult, A.max)
+        times(2, "cy")
+        wait("v", "cx")
+        limit(1, "cx")
+        wait("v", "cw")
+        times(3, "cy")
+        for s in range(1, 4):
             wait("v", "cv")
             u, z = T.bb[:, 60 * s + 2:60 * s + 60:3], T.d0a[:, 60 * s + 2:60 * s + 60:3]
-            tt(T.bb[:, 60 * s:60 * s + 60:3], u, part(T.ta, s), A.is_gt)
-            if s == 0:
-                fits(0)
-                tt(T.bb[:, 1:60:3], u, part(T.n1, 0), A.add, "cw")
-                ts(T.v0[:], u0, -12.0, A.add, sem="cw")
-                fits(1)
-                wait("v", "cv")
-                tt(z, part(T.gk, 0), T.bb[:, 0:60:3], A.is_ge)
-                wait("v", "cw")
-                times(1)
-                fits(2)
-            else:
-                tt(T.bb[:, 60 * s + 1:60 * s + 60:3], u, part(T.n1, s), A.add)
-                wait("v", "cw")
-                tt(z, u, part(T.thr, s), A.is_le)
-                if s == 1:
-                    limit(2)
-                    times(3)
-                if s == 3 and t == 0:
-                    wait("v", kn2)
-                    tt(T.c1[:, 0:20], T.iz2[:, 0:20], T.npk[:, 0:40:2], A.subtract, "cw")
-                    tt(T.c1[:, 20:40], T.iz2[:, 20:40], T.npk[:, 0:40:2], A.add, "cw")
-            wait("v", "cv")
-            scan(T.bb[:, 60 * s + 60:60 * s + 120], T.d0a[:, 60 * s:60 * s + 60], T.bb[:, 60 * s:60 * s + 60], A.mult, A.max)
-            if s < 2:
-                wait("v", "cw")
-            if s == 0:
-                limit(1)
-                times(2)
-                fits(3)
+            buf, o = (T.bb, 60 * s) if s < 3 else (T.b3, 0)
+            tt(buf[:, o:o + 60:3], u, part(T.ta, s), A.is_gt)
+            tt(buf[:, o + 1:o + 60:3], u, part(T.n1, s), A.add)
+            wait("v", "cx", "cw")
+            tt(z, u, part(T.thr, s), A.is_le)
             if s == 1:
-                limit(3)
-        bar("v")
-        tt(T.yy[:], T.bb[:, 62:300:3], T.d0a[:, 2:240:3], A.mult)
+                wait("v", "cy")
+                limit(2, "cw")
+                limit(3, "cw")
+            if s == 2 and t == 0:
+                wait("v", kn2)
+                tt(T.c1[:, 0:20], T.iz2[:, 0:20], T.npk[:, 0:40:2], A.subtract, "cx")
+                tt(T.c1[:, 20:40], T.iz2[:, 20:40], T.npk[:, 0:40:2], A.add, "cx")
+            if s == 3:
+                tt(T.yb[:, 2:180:3], T.bb[:, 62:240:3], T.d0a[:, 2:180:3], A.mult, "cw")
+            wait("v", "cv")
+            scan(T.bb[:, 60 * s + 60:60 * s + 120] if s < 3 else T.yb[:, 180:240], T.d0a[:, 60 * s:60 * s + 60], buf[:, o:o + 60], A.mult, A.max)
+            if s == 3 and t == 0:
+                wait("v", kfl)
+                scan(T.wsc[:], T.lift[:], T.flg[:], A.add, A.max, sem="cx")
         nz = T.npk[:, 0:40:2]
-        bar("v")
-        wait("v", krp)
+        wait("v", "cv", "cw", krp)
         ksn = tok()
-        tt(ab[:, 40:88], T.yy[:].indirect(T.plo[:, 0:3]), T.u0r[:], A.subtract, ksn)
-        tt(ab[:, 0:40], T.r1r[:], T.yy[:, 1:80:2], A.subtract, ksn)
+        tt(ab[:, 40:88], T.yb[:].indirect(T.plo[:, 0:3]), T.u0r[:], A.subtract, ksn)
+        tt(ab[:, 0:40], T.r1r[:], T.yb[:, 5:240:6], A.subtract, ksn)
+        if t == 0:
+            tt(T.jj[:, 0:250:2], T.ge[:], T.ii[:, 125:250], A.add, "cw")
         wait("g", ksn)
         send(lb[:], ab[:, 0:80], "rb%d" % t, dst)
-        bar("v")
+        wait("v", ksn)
         az, sz_, ok1, ok2, ok = ab[:, 40:80:2], ab[:, 0:40:2], T.sm[:, 0:20], T.sm[:, 20:40], T.sm[:, 40:60]
         tt(T.x1[:, 0:20], az, T.c1[:, 0:20], A.add)
         tt(T.x1[:, 20:40], sz_, T.c1[:, 20:40], A.add)
@@ -354,80 +391,73 @@ def rank_program(g, core, T, topo):
         wait("a", kzl, kth)
         kgm = act(T.mz[:, 160:320], win.indirect(T.zl[:, 10:20]), sem=tok())
         if t == 0:
-            wait("a", k6)
-            kfl = tok()
-            act(T.flg[:, 0:250:2], T.ii[:, 375:500], sem=kfl)
-            act(T.flg[:, 1:250:2], T.ii[:, 375:500], 1.0, 20.0, sem=kfl)
-            act(T.lift[:, 160:256], T.lift[:, 0:96], sem=kfl)
-            for ap, n in ((T.flg[:, 250:256], 6), (T.jj[:, 250:256], 6), (T.val[:, 250:256], 6), (T.fe[:, 40:48], 8)):
-                zero(ap, n, kfl)
-            khz = zero(T.hh[:, 0:800:2], 400, tok())
+            khz = tok()
+            for ap, n in ((T.jj[:, 250:256], 6), (T.val[:, 250:256], 6), (T.fe[:, 40:48], 8), (T.hh[:, 0:800:2], 400)):
+                zero(ap, n, khz)
         kt01 = tok()
         for b in range(2):
             act(T.t01[:, C * b:C * b + C], T["pd%d" % b][:, 0:C], sem=kt01)
-        wait("v", kzl, kth)
-        cp(T.mz[:, 0:160], win.indirect(T.zl[:, 0:10]))
-        bar("v")
-        tt(T.zt[:, 0:160], win.indirect(T.zl[:, 20:30]), T.mz[:, 0:160], A.add)
-        wait("v", kgm)
-        tt(T.zt[:, 160:320], win.indirect(T.zl[:, 30:40]), T.mz[:, 160:320], A.add)
-        bar("v")
+        wait("v", kzl, kth, "cx")
+        cp(T.mz[:, 0:64], win.indirect(T.zl[:, 0:4]))
+        cp(T.mz[:, 64:160], win.indirect(T.zl[:, 4:10]), "cx")
+        wait("v", "cv", "cw")
+        tt(T.zt[:, 0:64], win.indirect(T.zl[:, 20:24]), T.mz[:, 0:64], A.add)
+        wait("v", "cx", kgm)
+        tt(T.zt[:, 64:320], win.indirect(T.zl[:, 24:40]), T.mz[:, 64:320], A.add)
+        if t == 0:
+            ts(T.glo[:], T.wsc[:, 15:256:16], fix, A.subtract, sem="cw")
+        wait("v", "cv")
         kqz = quant(lq[:, K:K + 128], ls[:, K:K + 128], T.zt[:], tok())
         wait("g", kqz)
         send(lq[:, 0:K].bitcast(dt.uint8), lq[:, K:2 * K].bitcast(dt.uint8), "rc%d" % t, dst)
         send(ls[:, 0:K], ls[:, K:2 * K], "rs%d" % t, dst)
 
-        if t == 0:
-            wait("v", k6)
-            ts(T.ge[:], T.ii[:, 0:125], qc, A.add, 20.0, A.is_ge)
-            bar("v")
-            tt(T.jj[:, 0:250:2], T.ge[:], T.ii[:, 125:250], A.add)
-            ts(T.gt[:], T.ge[:], -40.0, A.mult, T.cola[:, 4:5], A.add)
-            wait("v", kfl)
-            wrap(T.glo[:], T.flg[:], 256)
-            cp(T.jj[:, 1:250:2], T.jj[:, 0:250:2])
-            tt(T.val[:, 0:250:2], T.gt[:], T.ii[:, 250:375], A.add)
-            bar("v")
-            ts(T.val[:, 1:250:2], T.val[:, 0:250:2], -1.0, A.add)
-            ms(T.jj[:, 0:250:10], 1000.0)
-            ms(T.jj[:, 1:250:10], 1000.0)
-        if t == 1:
-            wait("v", dv, kfo)
-            kv = quant(T.qv[:], T.sv[:], T.vin[:], tok())
-            kol = wrap(T.olo[:], T.flo[:], 160, sem=tok())
-        if t == 2:
-            tt(T.o1[:, 0:20], az, nz, A.subtract)
-            tt(T.o1[:, 20:40], sz_, nz, A.add)
-            tt(ok, ok1, ok2, A.mult)
-            bar("v")
-            tt(T.o1[:, 40:60], T.o1[:, 0:20], sz_, A.max)
-            tt(T.o1[:, 60:80], T.o1[:, 20:40], az, A.min)
-            bar("v")
-            tt(T.o2[:, 0:20], T.o1[:, 40:60], ok, A.mult)
-            ts(T.o1[:, 80:100], T.o1[:, 60:80], -1.0, A.add)
-            bar("v")
-            tt(T.o2[:, 20:40], T.o1[:, 80:100], ok, A.mult)
-            bar("v")
-            wait("a", cp(T.oo[:], T.o2[:], tok()), kol)
-            act(T.orep[:], T.tab[:].indirect(T.oo[:]), 1.0, -1.0)
-            bar("a")
-            wait("y", act(T.obt[:], T.orep[:].indirect(T.olo[:]), sem=tok()))
-            dma("y", T.ob[:], T.obt[0:128:16, :])
-
         ng, ag, sg = T["ng%d" % (t % 2)][:], lb[:, 41:80:2], lb[:, 1:40:2]
+        if t == 0:
+            cp(T.jj[:, 1:250:2], T.jj[:, 0:250:2], "cw")
+            tt(T.val[:, 0:250:2], T.gt[:], T.ii[:, 250:375], A.add, "cw")
+        if t == 1:
+            wait("v", dw, kfo)
+            kv = quant(T.qv[:], T.sv[:], T.vin[:], tok())
+            scan(T.wsc[:, 0:160], T.lift[:, 0:160], T.flo[:], A.add, A.max, sem="cw")
+        if t == 2:
+            tt(T.o1[:, 0:20], az, nz, A.subtract, "cw")
+            tt(T.o1[:, 20:40], sz_, nz, A.add, "cw")
+            tt(ok, ok1, ok2, A.mult, "cw")
         wait("v", "rn%d" % (t % 2), "rb%d" % t)
         tt(T.f1[:, 0:20], ag, ng, A.subtract)
         tt(T.f1[:, 20:40], sg, ng, A.add)
-        bar("v")
+        wait("v", "cw")
+        if t == 0:
+            ts(T.val[:, 1:250:2], T.val[:, 0:250:2], -1.0, A.add, sem="cw")
+            ms(T.jj[:, 0:250:10], 1000.0, "cw")
+            ms(T.jj[:, 1:250:10], 1000.0, "cw")
+        if t == 1:
+            kol = ts(T.olo[:], T.wsc[:, 15:160:16], fix, A.subtract, sem=tok())
+        if t == 2:
+            tt(T.o1[:, 40:60], T.o1[:, 0:20], sz_, A.max, "cw")
+            tt(T.o1[:, 60:80], T.o1[:, 20:40], az, A.min, "cw")
+        wait("v", "cv")
         tt(T.fe[:, 0:20], T.f1[:, 0:20], sg, A.max)
         tt(T.f1[:, 40:60], T.f1[:, 20:40], ag, A.min)
-        bar("v")
+        if t == 2:
+            wait("v", "cw")
+            tt(T.o2[:, 0:20], T.o1[:, 40:60], ok, A.mult, "cw")
+            ts(T.o1[:, 80:100], T.o1[:, 60:80], -1.0, A.add, sem="cw")
+        wait("v", "cv")
         tt(T.fe[:, 20:40], T.f1[:, 40:60], T.fe[:, 0:20], A.max)
+        if t == 2:
+            wait("v", "cw")
+            tt(T.o2[:, 20:40], T.o1[:, 80:100], ok, A.mult, "cw")
         bar("v")
+        wait("v", khz)
         tt(T.nf[:], T.fe[:].indirect(T.glo[:]), T.jj[:], A.is_gt)
-        bar("v")
+        if t == 2:
+            wait("a", cp(T.oo[:], T.o2[:], tok()), kol)
+            kor = act(T.orep[:], T.tab[:].indirect(T.oo[:]), 1.0, -1.0, sem=tok())
+        wait("v", "cv")
         scan(T.gs[:], T.nf[:], T.val[:], A.mult, A.max)
-        bar("v")
+        wait("v", "cv")
         kel = cp(T.el[:, 0:25], T.gs[:, 9:250:10], tok())
 
         wait("p", dw, kqz, "rc%d" % t, "rs%d" % t)
@@ -445,39 +475,45 @@ def rank_program(g, core, T, topo):
         kg2 = act(T.g2[:], hw[2].indirect(el), sem=tok())
         wait("a", kh3)
         kg3 = act(T.g3[:], hw[3].indirect(el), sem=tok())
-        bar("v")
+        if t == 2:
+            wait("a", kor)
+            kob = act(T.obt[:], T.orep[:].indirect(T.olo[:]), sem=tok())
         for b in range(2):
             wait("v", kh[b])
             ts(T.hh[:, 200 * b + 1:200 * b + 160:2], T["ph%d" % b][:, 0:K], 0.03125, A.mult, sem=W2[b])
-        wait("v", khz, kt01)
+        wait("v", kt01, kel)
         for b in range(2):
             wait("v", W2[b])
             tt(T.xn[:, b:1600:4], hw[b].indirect(el), T.t01[:, C * b:C * b + C], A.add)
         wait("v", kg2)
         tt(T.xn[:, 2:1600:4], T.g2[:], T.pd2[:, 0:C], A.add)
         wait("v", kg3)
-        for h in range(2):
-            tt(T.xn[:, 800 * h + 3:800 * h + 800:4], halves(T.g3, 200)[h], T.pd3[:, 200 * h:200 * h + 200], A.add, W2[h])
+        for h, (a, b) in enumerate(CUT if t < R - 1 else END):
+            tt(T.xn[:, 4 * a + 3:4 * b:4], T.g3[:, a:b], T.pd3[:, a:b], A.add, W2[h])
         xs = T.xn
 
+    wait("y", kob)
+    dout = dma("y", T.ob[:], T.obt[0:128:16, :])
     wait("p", kv)
     kx, ky = [], []
-    for h in range(2):
+    for h, (a, b) in enumerate(END):
         wait("v", W2[h])
-        q, s_ = halves(T.qx, 200)[h], halves(T.sx, 200)[h]
-        kx.append(quant(q, s_, halves(xs, 800)[h], tok()))
-        wait("p", kx[h])
-        ky.append(mm(T["ph%d" % h][:, 0:200], T.qv[:], T.sv[:], q, s_))
+        k_, s_ = scores(h, END, xs, T.qv, T.sv)
+        kx.append(k_)
+        ky.append(s_)
     wait("y", *kx)
-    dma("y", T.oc[:], T.qx[:].bitcast(dt.uint8))
+    dma("y", T.oc[:], T.qx[:].bitcast(dt.uint8), dout)
+    wait("a", *kx)
+    for k in range(2):
+        dma("a", T.osc[4 * k:4 * k + 4, :], T.sx[32 * k:32 * k + 4, :], dout)
     wait("v", ky[0])
-    wait("y", cp(T.yt[:, 0:200], T.ph0[:, 0:200], tok()))
-    dma("y", T.y[:, 0:200], T.yt[:, 0:200])
-    wait("v", ky[1])
-    wait("a", cp(T.yt[:, 200:400], T.ph1[:, 0:200], tok()))
-    dma("a", T.y[:, 200:400], T.yt[:, 200:400])
-    for k in range(4):
-        dma("a" if k % 2 else "y", T.osc[4 * k:4 * k + 4, :], T.sx[32 * k:32 * k + 4, :])
+    wait("y", cp(T.yt[:, 0:272], sb[0][:, 0:272], tok()))
+    dma("y", T.y[:, 0:272], T.yt[:, 0:272], dout)
+    wait("a", ky[1])
+    wait("a", act(T.yt[:, 272:400], sb[1][:, 0:128]))
+    dma("a", T.y[:, 272:400], T.yt[:, 272:400], dout)
+    for k in range(2, 4):
+        dma("a" if k == 2 else "y", T.osc[4 * k:4 * k + 4, :], T.sx[32 * k:32 * k + 4, :], dout)
     for s in list(total):
         if max([seen.get((q, s), 0) for q in qs]) < total[s]:
             wait("g", s)

from concourse.mybir import dt, AluOpType as A, ActivationFunctionType as F

C, K, R = 400, 80, 3
STEP = [1, 2, 1]
BIG = 1e29
CUT = [(0, 200), (200, 400)]
END = [(0, 272), (272, 400)]
Q4, U8, BF, F32, I32, U16 = "float8_e4m3fn_x4", "uint8", "bfloat16", "float32", "int32", "uint16"
SCRATCH = {}
for _d, _l in (
    (BF, "xin 1600 xn 1600 uin 512 vin 512 ones 128 eb 516 zt 512 mz 320 th 1616 t01 800 reset 200 nn 400 key 400 vv 400 n1g 20 ng0 20 ng1 20 "
         "snd0 88 snd1 88 snd2 88 lb0 80 lb1 80 lb2 80"),
    (Q4, "qx 400 qu 128 qu2 128 qv 128 qw 512 qe 512 lq0 208 lq1 208 lq2 208"),
    (U8, "sx 400 su 128 su2 128 sv 128 sw 512 se 512 ls0 208 ls1 208 ls2 208"),
    (I32, "bli 8 pi 1 qi 3 upi 8"),
    (U16, "upo 8 blo 8 lno 10 nlo 40 plo 4 glo 16 olo 10 el 26 zl 40 oo 40"),
    (F32, "hh 800 g2 400 g3 400 yt 400 ex 400 qf 3 cola 8 colb 8 tab 32 t16 160 lift 256 il 10 xg 10 ln 10 a80 80 c640 640 hn 640 npk 40 "
          "ns 80 n1 80 ta 80 n12 80 st 40 d0a 240 c1 40 iz 20 iz2 40 flp 48 flg 256 flo 160 wsc 256 ii 500 sg 125 ge 125 gt 125 jj 256 val 256 "
          "nf 256 gs 256 cand 160 hs 160 gk 80 pv 80 thr 80 v0 20 bb 240 b3 60 yb 240 u0r 48 r1r 40 x1 40 sm 60 fe 48 f1 60 w1 40 ww 40 "
          "o1 120 o2 40 orep 640 obt 160"),
):
    _w = _l.split()
    for _i in range(0, len(_w), 2):
        SCRATCH[_w[_i]] = ("sbuf", [128, int(_w[_i + 1])], _d)
for _b in range(4):
    SCRATCH["pd%d" % _b] = ("psum", [128, 512], F32)
    SCRATCH["ph%d" % _b] = ("psum", [128, 512], F32)
SEMAPHORES = ["cv", "cw", "cx", "cy", "ca", "sent", "rn0", "rn1"] + ["r%s%d" % (n, t) for n in "bcs" for t in range(R)] + ["s%d" % i for i in range(133)]


def rank_program(g, core, T, topo):
    rank = T.rank_of(core)
    if rank is None:
        return
    V, S, P, Y = g.vector, g.scalar, g.tensor, g.sync
    qs = {"v": V, "a": S, "p": P, "y": Y, "g": g}
    total, seen, pend, nxt = {}, {}, {"v": [], "a": [], "g": []}, [0]
    W2 = ["cv", "cw"]

    def tok():
        nxt[0] += 1
        return SEMAPHORES[16 + nxt[0]]

    def op(q, ins, sem=None, n=1):
        sem = sem or "c" + q
        ins.then_inc(T.sem[sem], n)
        total[sem] = total.get(sem, 0) + n
        if q in pend and n == 1 and sem not in pend[q]:
            pend[q].append(sem)
        return sem

    def wait(q, *sems):
        for s in sems:
            if seen.get((q, s), 0) < total[s]:
                qs[q].wait_ge(T.sem[s], total[s])
                seen[(q, s)] = total[s]

    def bar(q):
        wait(q, *pend[q])
        pend[q][:] = []

    def ms(ap, c, sem=None):
        return op("v", V.memset(ap, c), sem)

    def ts(out, a, s1, o1, s2=None, o2=None, sem=None):
        return op("v", V.tensor_scalar(out, a, s1, None, o1) if o2 is None else V.tensor_scalar(out, a, s1, s2, o1, o2), sem)

    def tt(out, a, b, o, sem=None):
        return op("v", V.tensor_tensor(out, a, b, o), sem)

    def cp(out, a, sem=None):
        return op("v", V.tensor_copy(out, a), sem)

    def scan(out, a, b, o0, o1, init=0.0, sem=None):
        return op("v", V.tensor_tensor_scan(out, a, b, init, o0, o1), sem)

    def quant(q, s, a, sem=None):
        return op("v", V.quantize_mx(q, s, a), sem)

    def act(out, a, scale=1.0, bias=0.0, func=F.Identity, sem=None):
        return op("a", S.activation(out, a, func, bias=bias, scale=scale), sem)

    def zero(out, n, sem):
        return act(out, T.key[:, 0:n], 0.0, sem=sem)

    def iota(out, pattern, base, sem, ch=0, whole=False):
        if whole:
            return op("g", g.iota(out, pattern, base, ch), sem)
        return op("g", g.iota(out, pattern, base, ch, allow_small_or_imprecise_dtypes=True), sem)

    def mm(out, lq, ls, rq, rs):
        return op("p", P.matmul_mx(out, lq, ls, rq, rs, True, True), tok())

    def dma(q, out, a, sem=None):
        return op(q, qs[q].dma_start(out, a), sem or tok(), 16)

    def send(out, a, sem, dst):
        rid, pid, _ = topo.addr(dst)
        g.remote_dma(out, a, T.sem[sem], T.sem.sent, pid, rid, topo.mask(core, dst))
        total["sent"] = total.get("sent", 0) + len(topo.engines(core, dst))
        total[sem] = len(topo.engines(dst, core))

    db = dma("a", T.bli[:, 0:5], T.bl[:])
    du = dma("a", T.uin[:], T.u[:])
    dx = [dma("y", T.xin[:, 4 * a:4 * b], T.x[:, 4 * a:4 * b]) for a, b in CUT]
    dw = dma("y", T.qw[:].bitcast(dt.uint8), T.wc[:])
    dma("y", T.sw[:], T.ws[:], dw)
    dma("y", T.vin[:], T.v[:], dw)

    k0, k1, k2, k3, k4, k5, k6 = [tok() for _ in range(7)]
    iota(T.pi[:], [[0, 1]], 0, k0, ch=1, whole=True)
    iota(T.upi[:], [[16, 8]], 0, k0, whole=True)
    iota(T.il[:, 0:5], [[4, 5]], 0, k0)
    iota(T.il[:, 5:10], [[-4, 5]], 20, k0)
    iota(T.tab[:], [[1, 32]], 0, k1)
    iota(T.t16[:], [[0, 10], [1, 16]], 0, k2)
    ko = ms(T.ones[:], 1.0, tok())
    ms(T.eb[:], 0.0, ko)
    ms(T.flp[:], 0.0, ko)
    ms(T.reset[:], 0.0)
    ms(T.ex[:, 0:400:200], BIG)
    ms(T.b3[:], 0.0)
    ms(T.yb[:], 0.0)
    wait("g", ko)
    op("g", g.affine_select(T.eb[:, 3:515:4], T.ones[:], [[1, 128]], A.is_equal, 0.0, 0, -1), k3)
    iota(T.flp[:, 0:40], [[-60, 4], [6, 10]], 182, k5)
    iota(T.iz[:], [[0, 4], [80, 5]], -400, k5)
    iota(T.key[:], [[0, 20], [-1, 20]], 32, k4)

    wait("v", k0)
    ts(T.qi[:, 0:1], T.pi[:], 15, A.bitwise_and)
    ts(T.qi[:, 1:2], T.pi[:], 2, A.logical_shift_right, 3, A.bitwise_and)
    ts(T.qi[:, 2:3], T.pi[:], 3, A.bitwise_and)
    kup = cp(T.upo[:], T.upi[:], tok())
    wait("v", "cv")
    kq = cp(T.qf[:], T.qi[:], tok())
    ms(T.reset[:, 0:200:20], BIG, "cw")
    wait("v", kq)
    qc, rc, bc = T.qf[:, 0:1], T.qf[:, 1:2], T.qf[:, 2:3]
    ts(T.xg[:, 0:5], T.il[:, 5:10], qc, A.add)
    ts(T.ln[:, 0:10:2], T.il[:, 0:5], rc, A.add, sem="cw")
    wait("v", "cv")
    ts(T.xg[:, 5:10], T.xg[:, 0:5], 20.0, A.is_ge, -20.0, A.mult)
    wait("v", k2)
    kt = ms(T.t16[:, 0:160:16], -1000.0, tok())
    wait("v", "cv")
    tt(T.ln[:, 1:10:2], T.xg[:, 0:5], T.xg[:, 5:10], A.add)
    wait("v", db)
    kb = cp(T.blo[:, 0:5], T.bli[:, 0:5], tok())
    wait("v", "cv", "cw")
    knl = tok()
    for k in range(4):
        ts(T.nlo[:, 10 * k:10 * k + 10], T.ln[:], 4.0, A.mult, float(3 - k), A.add, knl)
    ts(T.lno[:], T.ln[:], 20.0, A.mult, 19.0, A.add)
    wait("v", du)
    kqu = quant(T.qu[:], T.su[:], T.uin[:], tok())
    wait("v", k3)
    ke = tok()
    for b in range(2):
        quant(T.qe[:, 128 * b:128 * b + 128], T.se[:, 128 * b:128 * b + 128], T.eb[:, 3 - b:515 - b], ke)
    wait("v", kqu, kup)
    kpu = cp(T.qu2[:].bitcast(dt.uint32), T.qu[:].bitcast(dt.uint32).indirect(T.upo[:]), tok())

    wait("a", kq)
    kc = tok()
    act(T.cola[:, 1:2], qc, -32.0, 480.0, F.Square)
    act(T.cola[:, 0:1], qc, -2048.0, -1024.0)
    act(T.cola[:, 2:3], rc, 20.0, -1.0, sem=kc)
    act(T.cola[:, 3:4], bc, 1.0, 1600.0, sem=kc)
    act(T.cola[:, 4:5], qc, 2.0, 0.0, sem=kc)
    act(T.colb[:, 3:4], rc, 20.0, -2.0, sem=kc)
    act(T.cola[:, 5:6], qc, 1.0, -19.5, sem=kc)
    wait("a", "ca", kt)
    fix = T.cola[:, 1:2]
    act(T.lift[:, 0:160], T.t16[:], 2048.0, T.cola[:, 0:1], sem=kc)
    for j, sc, bi in ((0, -1.0, 0.0), (1, 1.0, 45.0)):
        act(T.colb[:, j:j + 1], fix, sc, bi, sem=kc)
    wait("a", k1, kb)
    act(T.a80[:], T.tab[:].indirect(T.blo[:, 0:5]))
    for j, bi in ((2, 67.0), (4, 32.0), (5, 13.0), (6, 12.0), (7, 33.0)):
        act(T.colb[:, j:j + 1], fix, 1.0, bi, sem=kc)
    wait("a", kup, kqu)
    op("a", S.activation(T.su2[:], T.su[:].indirect(T.upo[:]), F.Copy), kpu)
    wait("a", "ca", knl)
    kc6 = act(T.c640[:], T.a80[:].indirect(T.nlo[:]), sem=tok())
    wait("a", k4)
    kn = zero(T.d0a[:, 0:240:3], 80, tok())

    xs = T.xin
    sb = [T.ph3, T.ph2]

    def scores(h, cut, src, side, sc):
        a, b = cut[h]
        k = quant(T.qx[:, a:b], T.sx[:, a:b], src[:, 4 * a:4 * b], tok())
        wait("p", k)
        return k, mm(sb[h][:, 0:b - a], side[:], sc[:], T.qx[:, a:b], T.sx[:, a:b])

    for t in range(R):
        dst = T.cores[rank ^ STEP[t]]
        lq, ls, lb, ab = [T["%s%d" % (n, t)] for n in ("lq", "ls", "lb", "snd")]

        if t == 0:
            wait("p", kpu)
        ks = []
        for h in range(2):
            wait("v", dx[h] if t == 0 else W2[h])
            ks.append(scores(h, CUT, xs, T.qu2, T.su2)[1])
        if t == 0:
            for b in range(2, 4):
                quant(T.qe[:, 128 * b:128 * b + 128], T.se[:, 128 * b:128 * b + 128], T.eb[:, 3 - b:515 - b], ke)
            wait("p", ke)
            wait("v", "cv", "cw")
        kd = [mm(T["pd%d" % b][:, 0:C], T.qe[:, 128 * b:128 * b + 128], T.se[:, 128 * b:128 * b + 128], T.qx[:], T.sx[:]) for b in range(4)]

        for h, (a, b) in enumerate(CUT):
            wait("v", ks[h])
            scan(T.ex[:, a + 1:b], sb[h][:, 0:b - a - 1], T.reset[:, 1:b - a], A.min, A.add, BIG, W2[h])
        if t == 0:
            wait("v", kc6, kc)
            khn = tok()
            for k in range(4):
                scan(T.hn[:, 160 * k:160 * k + 160], T.lift[:, 0:160], T.c640[:, 160 * k:160 * k + 160], A.add, A.max, sem=khn)
            wait("a", khn, k5, kc)
            nfx = T.colb[:, 0:1]
            act(T.ns[:, 1:80:2], T.hn[:, 15:640:16], 1.0, nfx)
            for s in range(4):
                act(T.ns[:, 20 * s:20 * s + 20:2], T.hn[:, 160 * (3 - s) + 15:160 * (4 - s):16], 1.0, nfx)
            kng = act(T.n1g[:], T.hn[:, 31:640:32], 1.0, nfx, sem=tok())
            kn2 = act(T.npk[:], T.hn[:, 15:640:16], 1.0, nfx, sem=tok())
            wait("a", "ca")
            nl, nr = T.ns[:, 0:20:2], T.ns[:, 1:20:2]
            kst = tok()
            for j, (src, sc, col) in enumerate([(nl, -1.0, 4), (nr, 1.0, 5), (nl, 1.0, 6), (nr, -1.0, 7)]):
                act(T.st[:, 10 * j:10 * j + 10], src, sc, T.colb[:, col:col + 1], sem=kst)
            act(T.n12[:], T.ns[:], 1.0, 12.0, sem=kn)
            act(T.n1[:], T.ns[:], 1.0, 1.0, sem=kn)
            act(T.d0a[:, 1:240:3], T.ns[:], 1.0, 34.0, sem=kn)
            act(T.ta[:], T.ns[:], -1.0, 32.0, sem=kn)
            act(T.iz2[:, 0:20], T.iz[:], 1.0, T.cola[:, 2:3], sem=kn2)
            act(T.iz2[:, 20:40], T.iz[:], 1.0, T.colb[:, 3:4], sem=kn2)
            iota(T.ii[:, 0:125], [[0, 5], [-4, 5], [0, 5]], 20, k6)
            iota(T.ii[:, 125:250], [[4, 5], [1, 5], [0, 5]], 0, k6)
            iota(T.ii[:, 250:375], [[0, 5], [-8, 5], [-40, 5]], 181, k6)
            iota(T.ii[:, 375:500], [[0, 5], [1, 5], [-5, 5]], 20, k6)
            wait("g", kng)
            for j in range(2):
                send(T["ng%d" % j][:], T.n1g[:], "rn%d" % j, T.cores[rank ^ STEP[j]])
            kfo = iota(T.flo[:], [[4, 20], [-80, 4], [320, 2]], 240, tok())
        kth = tok()
        if t:
            for b in range(2):
                wait("a", kd[b])
                act(T.th[:, b:1600:4], T["pd%d" % b][:, 0:C], 0.5, sem=kth)
        for h, (a, b) in enumerate(CUT):
            wait("v", W2[h])
            tt(T.nn[:, a:b], sb[h][:, 0:b - a], T.ex[:, a:b], A.is_ge, W2[h])
        if t == 0:
            wait("v", k4, k5)
        for h, (a, b) in enumerate(CUT):
            wait("v", W2[h])
            scan(T.vv[:, a:b], T.nn[:, a:b], T.key[:, a:b], A.mult, A.max, sem=W2[h])
        if t == 0:
            scan(T.wsc[:, 0:48], T.lift[:, 0:48], T.flp[:], A.add, A.max, sem="cx")
        wait("v", "cv", "cw")
        cp(T.cand[:, 0:96], T.vv[:].indirect(T.lno[:, 0:6]))
        cp(T.cand[:, 96:160], T.vv[:].indirect(T.lno[:, 6:10]), "cw")
        wait("v", "cv")
        khs = scan(T.hs[:, 0:96], T.lift[:, 0:96], T.cand[:, 0:96], A.add, A.max, sem=tok())
        wait("v", "cw")
        scan(T.hs[:, 96:160], T.lift[:, 0:64], T.cand[:, 96:160], A.add, A.max, sem=khs)
        if t == 0:
            wait("v", "cx")
            ts(T.plo[:, 0:3], T.wsc[:, 15:48:16], fix, A.subtract, sem="cx")
        hs = T.hs[:, 15:160:16]
        wait("a", khs)
        krp = tok()
        for k in range(4):
            act(T.u0r[:, 10 * k:10 * k + 10], hs, 1.0, T.colb[:, 0:1], sem=krp)
            act(T.r1r[:, 10 * k:10 * k + 10], hs, -1.0, T.colb[:, 2:3], sem=krp)
        if t == 0:
            zero(T.u0r[:, 40:48], 8, krp)
            wait("a", k6)
            kfl = tok()
            act(T.sg[:], T.ii[:, 0:125], 1.0, T.cola[:, 5:6], F.Sign)
            act(T.flg[:, 0:250:2], T.ii[:, 375:500], sem=kfl)
            act(T.flg[:, 1:250:2], T.ii[:, 375:500], 1.0, 20.0, sem=kfl)
            act(T.lift[:, 160:256], T.lift[:, 0:96], sem=kfl)
            zero(T.flg[:, 250:256], 6, kfl)
            wait("a", "ca")
            act(T.ge[:], T.sg[:], 0.5, 0.5, sem=kfl)
            act(T.gt[:], T.sg[:], -20.0, T.cola[:, 4:5], sem=kfl)
            zero(T.th[:, 1600:1616], 16, kth)
            zero(T.zt[:, 320:512], 192, kth)
        for b in range(2 if t else 0, 4):
            wait("a", kd[b])
            act(T.th[:, b:1600:4], T["pd%d" % b][:, 0:C], 0.5, sem=kth)

        def part(buf, s):
            return buf[:, 20 * s:20 * s + 20]
        u0 = T.bb[:, 2:60:3]

        def fits(s, sem):
            tt(part(T.gk, s), u0, part(T.n12, s), A.is_gt, sem)

        def times(s, sem):
            tt(part(T.pv, s), part(T.gk, s), T.v0[:], A.mult, sem)

        def limit(s, sem):
            tt(part(T.thr, s), part(T.pv, s), part(T.ta, s), A.add, sem)
        wait("v", khs)
        if t == 0:
            wait("v", kst)
        st = [T.st[:, 10 * j:10 * j + 10] for j in range(4)]
        ts(T.bb[:, 2:60:6], hs, fix, A.subtract, sem="cw")
        ts(T.bb[:, 5:60:6], hs, -1.0, A.mult, T.colb[:, 1:2], A.add, "cw")
        tt(T.bb[:, 0:60:6], hs, st[0], A.is_gt)
        tt(T.bb[:, 3:60:6], hs, st[1], A.is_lt)
        tt(T.gk[:, 0:20:2], hs, st[2], A.is_gt)
        tt(T.gk[:, 1:20:2], hs, st[3], A.is_lt)
        wait("v", "cw")
        if t == 0:
            wait("v", kn)
        fits(1, "cw")
        ts(T.v0[:], u0, -12.0, A.add, sem="cw")
        tt(T.bb[:, 1:60:3], u0, part(T.n1, 0), A.add, "cy")
        wait("v", "cv")
        tt(T.d0a[:, 2:60:3], part(T.gk, 0), T.bb[:, 0:60:3], A.is_ge)
        fits(2, "cy")
        wait("v", "cw")
        times(1, "cx")
        fits(3, "cw")
        wait("v", "cv", "cy")
        scan(T.bb[:, 60:120], T.d0a[:, 0:60], T.bb[:, 0:60], A.mult, A.max)
        times(2, "cy")
        wait("v", "cx")
        limit(1, "cx")
        wait("v", "cw")
        times(3, "cy")
        for s in range(1, 4):
            wait("v", "cv")
            u, z = T.bb[:, 60 * s + 2:60 * s + 60:3], T.d0a[:, 60 * s + 2:60 * s + 60:3]
            buf, o = (T.bb, 60 * s) if s < 3 else (T.b3, 0)
            tt(buf[:, o:o + 60:3], u, part(T.ta, s), A.is_gt)
            tt(buf[:, o + 1:o + 60:3], u, part(T.n1, s), A.add)
            wait("v", "cx", "cw")
            tt(z, u, part(T.thr, s), A.is_le)
            if s == 1:
                wait("v", "cy")
                limit(2, "cw")
                limit(3, "cw")
            if s == 2 and t == 0:
                wait("v", kn2)
                tt(T.c1[:, 0:20], T.iz2[:, 0:20], T.npk[:, 0:40:2], A.subtract, "cx")
                tt(T.c1[:, 20:40], T.iz2[:, 20:40], T.npk[:, 0:40:2], A.add, "cx")
            if s == 3:
                tt(T.yb[:, 2:180:3], T.bb[:, 62:240:3], T.d0a[:, 2:180:3], A.mult, "cw")
            wait("v", "cv")
            scan(T.bb[:, 60 * s + 60:60 * s + 120] if s < 3 else T.yb[:, 180:240], T.d0a[:, 60 * s:60 * s + 60], buf[:, o:o + 60], A.mult, A.max)
            if s == 3 and t == 0:
                wait("v", kfl)
                scan(T.wsc[:], T.lift[:], T.flg[:], A.add, A.max, sem="cx")
        nz = T.npk[:, 0:40:2]
        wait("v", "cv", "cw", krp)
        ksn = tok()
        tt(ab[:, 40:88], T.yb[:].indirect(T.plo[:, 0:3]), T.u0r[:], A.subtract, ksn)
        tt(ab[:, 0:40], T.r1r[:], T.yb[:, 5:240:6], A.subtract, ksn)
        if t == 0:
            tt(T.jj[:, 0:250:2], T.ge[:], T.ii[:, 125:250], A.add, "cw")
        wait("g", ksn)
        send(lb[:], ab[:, 0:80], "rb%d" % t, dst)
        wait("v", ksn)
        az, sz_, ok1, ok2, ok = ab[:, 40:80:2], ab[:, 0:40:2], T.sm[:, 0:20], T.sm[:, 20:40], T.sm[:, 40:60]
        tt(T.x1[:, 0:20], az, T.c1[:, 0:20], A.add)
        tt(T.x1[:, 20:40], sz_, T.c1[:, 20:40], A.add)
        tt(ok1, az, sz_, A.is_gt, "cw")
        wait("v", "cv")
        tt(ok2, T.x1[:, 0:20], T.x1[:, 20:40], A.is_le)
        wait("v", "cw")
        tt(T.w1[:, 0:20], T.x1[:, 0:20], ok1, A.mult)
        tt(T.w1[:, 20:40], T.x1[:, 20:40], ok1, A.mult, "cw")
        wait("v", "cv")
        tt(T.ww[:, 0:20], T.w1[:, 0:20], ok2, A.mult)
        wait("v", "cw")
        tt(T.ww[:, 20:40], T.w1[:, 20:40], ok2, A.mult, "cw")
        wait("v", "cv")
        kzl = ts(T.zl[:, 0:20], T.ww[:, 0:20], 4.0, A.mult, T.cola[:, 3:4], A.add, tok())
        wait("v", "cw")
        ts(T.zl[:, 20:40], T.ww[:, 20:40], 4.0, A.mult, T.cola[:, 3:4], A.add, "cw")

        win = T.th[:]
        wait("a", kzl, kth)
        kgm = act(T.mz[:, 160:320], win.indirect(T.zl[:, 10:20]), sem=tok())
        if t == 0:
            khz = tok()
            for ap, n in ((T.jj[:, 250:256], 6), (T.val[:, 250:256], 6), (T.fe[:, 40:48], 8), (T.hh[:, 0:800:2], 400)):
                zero(ap, n, khz)
        kt01 = tok()
        for b in range(2):
            act(T.t01[:, C * b:C * b + C], T["pd%d" % b][:, 0:C], sem=kt01)
        wait("v", kzl, kth, "cx")
        cp(T.mz[:, 0:64], win.indirect(T.zl[:, 0:4]))
        cp(T.mz[:, 64:160], win.indirect(T.zl[:, 4:10]), "cx")
        wait("v", "cv", "cw")
        tt(T.zt[:, 0:64], win.indirect(T.zl[:, 20:24]), T.mz[:, 0:64], A.add)
        wait("v", "cx", kgm)
        tt(T.zt[:, 64:320], win.indirect(T.zl[:, 24:40]), T.mz[:, 64:320], A.add)
        if t == 0:
            ts(T.glo[:], T.wsc[:, 15:256:16], fix, A.subtract, sem="cw")
        wait("v", "cv")
        kqz = quant(lq[:, K:K + 128], ls[:, K:K + 128], T.zt[:], tok())
        wait("g", kqz)
        send(lq[:, 0:K].bitcast(dt.uint8), lq[:, K:2 * K].bitcast(dt.uint8), "rc%d" % t, dst)
        send(ls[:, 0:K], ls[:, K:2 * K], "rs%d" % t, dst)

        ng, ag, sg = T["ng%d" % (t % 2)][:], lb[:, 41:80:2], lb[:, 1:40:2]
        if t == 0:
            cp(T.jj[:, 1:250:2], T.jj[:, 0:250:2], "cw")
            tt(T.val[:, 0:250:2], T.gt[:], T.ii[:, 250:375], A.add, "cw")
        if t == 1:
            wait("v", dw, kfo)
            kv = quant(T.qv[:], T.sv[:], T.vin[:], tok())
            scan(T.wsc[:, 0:160], T.lift[:, 0:160], T.flo[:], A.add, A.max, sem="cw")
        if t == 2:
            tt(T.o1[:, 0:20], az, nz, A.subtract, "cw")
            tt(T.o1[:, 20:40], sz_, nz, A.add, "cw")
            tt(ok, ok1, ok2, A.mult, "cw")
        wait("v", "rn%d" % (t % 2), "rb%d" % t)
        tt(T.f1[:, 0:20], ag, ng, A.subtract)
        tt(T.f1[:, 20:40], sg, ng, A.add)
        wait("v", "cw")
        if t == 0:
            ts(T.val[:, 1:250:2], T.val[:, 0:250:2], -1.0, A.add, sem="cw")
            ms(T.jj[:, 0:250:10], 1000.0, "cw")
            ms(T.jj[:, 1:250:10], 1000.0, "cw")
        if t == 1:
            kol = ts(T.olo[:], T.wsc[:, 15:160:16], fix, A.subtract, sem=tok())
        if t == 2:
            tt(T.o1[:, 40:60], T.o1[:, 0:20], sz_, A.max, "cw")
            tt(T.o1[:, 60:80], T.o1[:, 20:40], az, A.min, "cw")
        wait("v", "cv")
        tt(T.fe[:, 0:20], T.f1[:, 0:20], sg, A.max)
        tt(T.f1[:, 40:60], T.f1[:, 20:40], ag, A.min)
        if t == 2:
            wait("v", "cw")
            tt(T.o2[:, 0:20], T.o1[:, 40:60], ok, A.mult, "cw")
            ts(T.o1[:, 80:100], T.o1[:, 60:80], -1.0, A.add, sem="cw")
        wait("v", "cv")
        tt(T.fe[:, 20:40], T.f1[:, 40:60], T.fe[:, 0:20], A.max)
        if t == 2:
            wait("v", "cw")
            tt(T.o2[:, 20:40], T.o1[:, 80:100], ok, A.mult, "cw")
        bar("v")
        wait("v", khz)
        tt(T.nf[:], T.fe[:].indirect(T.glo[:]), T.jj[:], A.is_gt)
        if t == 2:
            wait("a", cp(T.oo[:], T.o2[:], tok()), kol)
            kor = act(T.orep[:], T.tab[:].indirect(T.oo[:]), 1.0, -1.0, sem=tok())
        wait("v", "cv")
        scan(T.gs[:], T.nf[:], T.val[:], A.mult, A.max)
        wait("v", "cv")
        kel = cp(T.el[:, 0:25], T.gs[:, 9:250:10], tok())

        wait("p", dw, kqz, "rc%d" % t, "rs%d" % t)
        kh = {}
        for b in (0, 2, 1, 3):
            kh[b] = mm(T["ph%d" % b][:, 0:128], T.qw[:, 128 * b:128 * b + 128], T.sw[:, 128 * b:128 * b + 128], lq[:, 0:128], ls[:, 0:128])
        el = T.el[:, 0:25]
        hw = [T.hh[:, 200 * b:200 * b + 200] for b in range(4)]
        bar("a")
        wait("a", kh[2])
        act(T.hh[:, 401:560:2], T.ph2[:, 0:K], 0.03125)
        wait("a", kh[3])
        kh3 = act(T.hh[:, 601:760:2], T.ph3[:, 0:K], 0.03125, sem=tok())
        wait("a", kel, "ca")
        kg2 = act(T.g2[:], hw[2].indirect(el), sem=tok())
        wait("a", kh3)
        kg3 = act(T.g3[:], hw[3].indirect(el), sem=tok())
        if t == 2:
            wait("a", kor)
            kob = act(T.obt[:], T.orep[:].indirect(T.olo[:]), sem=tok())
        for b in range(2):
            wait("v", kh[b])
            ts(T.hh[:, 200 * b + 1:200 * b + 160:2], T["ph%d" % b][:, 0:K], 0.03125, A.mult, sem=W2[b])
        wait("v", kt01, kel)
        for b in range(2):
            wait("v", W2[b])
            tt(T.xn[:, b:1600:4], hw[b].indirect(el), T.t01[:, C * b:C * b + C], A.add)
        wait("v", kg2)
        tt(T.xn[:, 2:1600:4], T.g2[:], T.pd2[:, 0:C], A.add)
        wait("v", kg3)
        for h, (a, b) in enumerate(CUT if t < R - 1 else END):
            tt(T.xn[:, 4 * a + 3:4 * b:4], T.g3[:, a:b], T.pd3[:, a:b], A.add, W2[h])
        xs = T.xn

    wait("y", kob)
    dout = dma("y", T.ob[:], T.obt[0:128:16, :])
    wait("p", kv)
    kx, ky = [], []
    for h, (a, b) in enumerate(END):
        wait("v", W2[h])
        k_, s_ = scores(h, END, xs, T.qv, T.sv)
        kx.append(k_)
        ky.append(s_)
    wait("y", *kx)
    dma("y", T.oc[:], T.qx[:].bitcast(dt.uint8), dout)
    wait("a", *kx)
    for k in range(2):
        dma("a", T.osc[4 * k:4 * k + 4, :], T.sx[32 * k:32 * k + 4, :], dout)
    wait("v", ky[0])
    wait("y", cp(T.yt[:, 0:272], sb[0][:, 0:272], tok()))
    dma("y", T.y[:, 0:272], T.yt[:, 0:272], dout)
    wait("a", ky[1])
    wait("a", act(T.yt[:, 272:400], sb[1][:, 0:128]))
    dma("a", T.y[:, 272:400], T.yt[:, 272:400], dout)
    for k in range(2, 4):
        dma("a" if k == 2 else "y", T.osc[4 * k:4 * k + 4, :], T.sx[32 * k:32 * k + 4, :], dout)
    for s in list(total):
        if max([seen.get((q, s), 0) for q in qs]) < total[s]:
            wait("g", s)
